import numpy as np
import ml_dtypes


def mxq(x, axis, fmt="e4m3"):
    dtype, down = {"e4m3": (ml_dtypes.float8_e4m3fn, 7), "e5m2": (ml_dtypes.float8_e5m2, 14)}[fmt]
    v = np.moveaxis(np.asarray(x, np.float32).astype(ml_dtypes.bfloat16).astype(np.float64), axis, -1)
    blocks = v.reshape(v.shape[:-1] + (-1, 32))
    amax = np.abs(blocks).max(-1, keepdims=True)
    byte = np.maximum(np.where(amax > 0, np.frexp(amax)[1] - 1 + 127, 0) - down, 1)
    scale = np.exp2(byte - 127.0)
    codes = (blocks / scale).astype(np.float32).astype(dtype).astype(np.float64)
    return np.moveaxis((codes * scale).reshape(v.shape), -1, axis)


WIDE = False


def mx_kscale(k):
    if not WIDE:
        return np.ones(k)
    levels = np.array([10, -10, 5, -5, 0])
    if k % 512:
        return np.exp2(np.random.permutation(np.resize(levels, k // 32))).repeat(32)
    a = np.empty((k // 512, 16))
    for p in range(k // 512):
        a[p, :8] = np.random.permutation(np.resize(levels, 8))
        for g in range(8):
            far = levels[np.abs(levels - a[p, g]) >= 10]
            a[p, g + 8] = far[np.random.randint(len(far))]
    return np.exp2(a.ravel()).repeat(32)


def f64(x):
    return np.asarray(x).astype(np.float64)


def striped(idx):
    return np.tile(idx.reshape(-1, 16).T, (8, 1)).astype(np.uint16)


def unstriped(offs):
    return offs[:16].T.reshape(-1).astype(np.int64)


def striped8(idx):
    return np.concatenate([x.reshape(-1, 16).T for x in idx]).astype(np.uint16)


def runs(offs, k):
    lists = np.stack([offs[16 * r : 16 * r + 16].T.reshape(-1) for r in range(8)]).astype(np.int64)
    return lists[np.arange(k) % 512 // 64]


def pack_weight(w):
    k, n = w.shape
    w = f64(np.asarray(w, np.float32).astype(ml_dtypes.bfloat16)).reshape(k // 32, 32, n)
    amax = np.abs(w).max(1)
    byte = np.clip(np.where(amax > 0, np.frexp(amax)[1] - 1 + 127 - 7, 1), 1, 254)
    scaled = (w * np.exp2(127.0 - byte)[:, None, :]).reshape(k, n).astype(np.float32)
    words = np.ascontiguousarray(scaled.reshape(k // 512, 128, 4, n).transpose(0, 1, 3, 2)).astype(ml_dtypes.float8_e4m3fn).view(np.uint8)
    return words, np.ascontiguousarray(byte.astype(np.uint8).reshape(k // 512, 16, n))


def unpack_weight(words, scales):
    g, p, n, _ = words.shape
    vals = np.ascontiguousarray(words).view(ml_dtypes.float8_e4m3fn).astype(np.float64) * np.repeat(np.exp2(scales.astype(np.float64) - 127.0), 8, axis=1)[..., None]
    return vals.transpose(0, 1, 3, 2).reshape(g * 512, n)


def silu(v):
    return v / (1.0 + np.exp(-np.maximum(v, -700.0)))

def planes(y):
    n, m = y.shape
    v = y.astype(np.float32).astype(ml_dtypes.bfloat16).astype(np.float64).reshape(n // 32, 32, m)
    top = np.abs(v).max(1)
    byte = np.clip(np.where(top > 0, np.frexp(top)[1] - 1 + 127 - 7, 1), 1, 254)
    codes = (v * np.exp2(127.0 - byte)[:, None, :]).reshape(n, m).astype(np.float32).astype(ml_dtypes.float8_e4m3fn).view(np.uint8)
    words = codes.reshape(n // 512, 128, 4, m).transpose(0, 1, 3, 2)
    return np.ascontiguousarray(words), np.ascontiguousarray(byte.astype(np.uint8).reshape(n // 512, 16, m))


K, T, S, N, H, U = 512, 2048, 512, 512, 512, 512


def setup_inputs():
    n = np.random.standard_normal
    s = mx_kscale(K)[:, None]
    u = mx_kscale(H)
    packed_xT = pack_weight(n((K, T)) * s)
    packed_w1 = pack_weight(n((K, H)) / np.sqrt(K) / s)
    packed_w2 = pack_weight(n((H, N)) / np.sqrt(H) / u[:, None])
    return {
        "x_words": packed_xT[0],
        "x_scales": packed_xT[1],
        "w1_words": packed_w1[0],
        "w1_scales": packed_w1[1],
        "gam": (np.random.uniform(0.5, 1.5, (H, U)) * u[:, None]).astype(np.float32),
        "bet": (n((H, U)) * u[:, None]).astype(np.float32),
        "res": n((N, S)).astype(np.float32),
        "w2_words": packed_w2[0],
        "w2_scales": packed_w2[1],
        "offs": striped(np.random.permutation(T)[:S]),
        "task": striped8(np.random.randint(0, U, (8, S))),
    }


def reference(x_words, x_scales, w1_words, w1_scales, gam, bet, res, w2_words, w2_scales, offs, task):
    xq = unpack_weight(x_words, x_scales)[:, unstriped(offs)]
    h = silu(unpack_weight(w1_words, w1_scales).T @ xq)
    z = h * (f64(gam)[np.arange(H)[:, None], runs(task, H)]) + f64(bet)[np.arange(H)[:, None], runs(task, H)]
    out_0 = f64(res) + (unpack_weight(w2_words, w2_scales).T @ mxq(z, 0, "e4m3"))
    return (out_0,) + planes(out_0)

@@ -1,0 +1,215 @@
+from contextlib import ExitStack
+
+import concourse.mybir as mybir
+
+F32 = mybir.dt.float32
+BF16 = mybir.dt.bfloat16
+I32 = mybir.dt.int32
+U32 = mybir.dt.uint32
+U16 = mybir.dt.uint16
+U8 = mybir.dt.uint8
+FP8X4 = mybir.dt.float8_e4m3fn_x4
+MULT = mybir.AluOpType.mult
+ADD = mybir.AluOpType.add
+SILU = mybir.ActivationFunctionType.Silu
+
+P = 128
+PACK = 4
+T, S, W = 2048, 512, 512
+HALF = 256
+UNIT = 128
+FLOPS = 2 * 2 * 512 * 512 * 512
+
+
+def tile_picked_filmres_silu_po_kernel(
+    tc, x_words, x_scales, w1_words, w1_scales, gam, bet, res, w2_words, w2_scales, offs, task, out_0, out_1, out_2
+):
+    nc = tc.nc
+
+    def words_of(dram):
+        return dram[0].rearrange("p n t -> p (n t)").bitcast(I32)
+
+    def rows_of(dram):
+        return dram.rearrange("(p t) c -> p t c", t=PACK)
+
+    def load_scale_rows(queue, plane, dram):
+        for q in range(4):
+            queue.dma_start(out=plane[32 * q : 32 * q + 4, :].bitcast(I32), in_=dram[0, 4 * q : 4 * q + 4, :].bitcast(I32))
+
+    def deal(dst, src):
+        nc.vector.tensor_copy(out=dst.rearrange("p (t m) -> p m t", t=PACK), in_=src.rearrange("p (m t) -> p m t", t=PACK))
+
+    with ExitStack() as ctx:
+        keep = ctx.enter_context(tc.tile_pool(name="keep", bufs=1))
+        psum = ctx.enter_context(tc.psum_pool(name="psum", bufs=1))
+
+        def tile(name, shape, dtype, tag=None):
+            return keep.tile(shape, dtype, name=name, tag=tag or name, align_bytes=64)
+
+        offs_t = tile("offs_t", [P, S // 16], U16)
+        task_t = tile("task_t", [P, S // 16], U16)
+        xw = tile("xw", [P, T], U32)
+        xs = tile("xs", [P, T], U8)
+        w1_raw = tile("w1_raw", [P, W], I32)
+        w2_raw = tile("w2_raw", [P, W], I32)
+        s1_raw = tile("s1_raw", [P, W], U8)
+        s2_raw = tile("s2_raw", [P, W], U8)
+        gam_t = [tile("gam%d" % t, [P, W], F32) for t in range(PACK)]
+        bet_t = [tile("bet%d" % t, [P, W], F32) for t in range(PACK)]
+        res_t = [tile("res%d" % a, [P, PACK, HALF], F32) for a in range(2)]
+
+        nc.vector.memset(xs[:].bitcast(I32), 0)
+        nc.gpsimd.memset(s1_raw[:].bitcast(I32), 0)
+        nc.gpsimd.memset(s2_raw[:].bitcast(I32), 0)
+
+        nc.sync.dma_start(offs_t[:], offs)
+        nc.sync.dma_start(out=w1_raw[:], in_=words_of(w1_words))
+        nc.sync.dma_start(out=xw[:].bitcast(I32)[:, 0 : T // 2], in_=words_of(x_words)[:, 0 : T // 2])
+        load_scale_rows(nc.sync, xs, x_scales)
+        nc.sync.dma_start(out=xw[:].bitcast(I32)[:, T // 2 : T], in_=words_of(x_words)[:, T // 2 : T])
+        load_scale_rows(nc.sync, s1_raw, w1_scales)
+        nc.sync.dma_start(task_t[:], task)
+        nc.sync.dma_start(out=w2_raw[:], in_=words_of(w2_words))
+        nc.sync.dma_start(out=gam_t[0][:], in_=rows_of(gam)[:, 0, :])
+        load_scale_rows(nc.sync, s2_raw, w2_scales)
+        for t in range(PACK):
+            if t + 1 < PACK:
+                nc.sync.dma_start(out=gam_t[t + 1][:], in_=rows_of(gam)[:, t + 1, :])
+            nc.sync.dma_start(out=bet_t[t][:], in_=rows_of(bet)[:, t, :])
+        for a in range(2):
+            nc.sync.dma_start(out=res_t[a][:], in_=rows_of(res)[:, :, a * HALF : (a + 1) * HALF])
+
+        xg_s = tile("xg_s", [P, S], U8)
+        xg_w = [tile("xg_w%d" % a, [P, HALF], U32) for a in range(2)]
+        w1 = tile("w1", [P, W], I32)
+        w2 = tile("w2", [P, W], I32)
+        s1 = tile("s1", [P, W], U8)
+        s2 = tile("s2", [P, W], U8)
+
+        nc.vector.tensor_copy(xg_s[:], xs[:].indirect(offs_t[:]))
+        deal(w1[:], w1_raw[:])
+        banks = [psum.tile([P, 512], F32, name="bank%d" % b) for b in range(8)]
+        h = [[tile("h%d_%d" % (a, t), [P, HALF], F32) for t in range(PACK)] for a in range(2)]
+        for a in range(2):
+            nc.vector.tensor_copy(xg_w[a][:], xw[:].indirect(offs_t[:, 16 * a : 16 * a + 16]))
+            if a == 0:
+                deal(s1[:], s1_raw[:])
+            for t in range(PACK):
+                acc = banks[PACK * a + t][:, 0:HALF]
+                nc.tensor.matmul_mx(
+                    out=acc,
+                    lhsT=w1[:, t * P : (t + 1) * P].bitcast(FP8X4),
+                    lhsT_scale=s1[:, t * P : (t + 1) * P],
+                    rhs=xg_w[a][:].bitcast(FP8X4),
+                    rhs_scale=xg_s[:, a * HALF : (a + 1) * HALF],
+                    start=True,
+                    stop=True,
+                )
+                nc.scalar.activation(out=h[a][t][:], in_=acc, func=SILU)
+        deal(s2[:], s2_raw[:])
+        deal(w2[:], w2_raw[:])
+
+        ring = [tile("ring%d" % i, [P, HALF], F32) for i in range(2)]
+        z = [tile("z0", [P, PACK, HALF], F32), tile("z1", [P, PACK, UNIT], F32), tile("z2", [P, PACK, UNIT], F32)]
+        starts = [0, HALF, HALF + UNIT]
+        widths = [HALF, UNIT, UNIT]
+        zq_w = tile("zq_w", [P, S], U32)
+        zq_s = tile("zq_s", [P, S], U8)
+        yq_w = tile("yq_w", [P, S], U32)
+        yq_s = tile("yq_s", [P, S], U8)
+        y = [tile("y%d" % u, [P, PACK, UNIT], F32) for u in range(4)]
+        zb, yb, prod = {}, {}, {}
+
+        def lists(c):
+            return task_t[:, starts[c] // 16 : (starts[c] + widths[c]) // 16]
+
+        def scale(c, t, dst):
+            prod[c, t] = dst
+            a, lo = divmod(starts[c], HALF)
+            nc.vector.tensor_tensor(dst, gam_t[t][:].indirect(lists(c)), h[a][t][:, lo : lo + widths[c]], MULT)
+
+        def shift(c, t):
+            nc.vector.tensor_tensor(z[c][:, t, :], bet_t[t][:].indirect(lists(c)), prod[c, t], ADD)
+
+        def round_z(u):
+            zb[u] = tile("zb%d" % u, [P, UNIT, PACK], BF16)
+            src = z[0][:, :, u * UNIT : (u + 1) * UNIT] if u < 2 else z[u - 1][:]
+            nc.scalar.copy(out=zb[u][:], in_=src.rearrange("p t j -> p j t"))
+
+        def second(u):
+            cols = slice(u * UNIT, (u + 1) * UNIT)
+            nc.vector.quantize_mx(out=zq_w[:, cols].bitcast(FP8X4), scales=zq_s[:, cols], in_=zb[u][:].rearrange("p j t -> p (j t)"))
+            for t in range(PACK):
+                nc.tensor.matmul_mx(
+                    out=banks[u][:, t * UNIT : (t + 1) * UNIT],
+                    lhsT=w2[:, t * P : (t + 1) * P].bitcast(FP8X4),
+                    lhsT_scale=s2[:, t * P : (t + 1) * P],
+                    rhs=zq_w[:, cols].bitcast(FP8X4),
+                    rhs_scale=zq_s[:, cols],
+                    start=True,
+                    stop=True,
+                )
+
+        def res_of(u):
+            return res_t[u // 2][:, :, (u % 2) * UNIT : (u % 2 + 1) * UNIT]
+
+        def finish(u, last=False):
+            cols = slice(u * UNIT, (u + 1) * UNIT)
+            nc.vector.tensor_tensor(y[u][:], banks[u][:].rearrange("p (t j) -> p t j", t=PACK), res_of(u), ADD)
+            nc.sync.dma_start(out=rows_of(out_0)[:, :, cols], in_=y[u][:])
+            yb[u] = tile("yb%d" % u, [P, UNIT, PACK], BF16)
+            if last:
+                nc.vector.tensor_copy(out=yb[u][:], in_=y[u][:].rearrange("p t j -> p j t"))
+            else:
+                nc.scalar.copy(out=yb[u][:], in_=y[u][:].rearrange("p t j -> p j t"))
+
+        def hand_on(u):
+            cols = slice(u * UNIT, (u + 1) * UNIT)
+            nc.vector.quantize_mx(out=yq_w[:, cols].bitcast(FP8X4), scales=yq_s[:, cols], in_=yb[u][:].rearrange("p j t -> p (j t)"))
+            nc.sync.dma_start(out=words_of(out_1)[:, cols], in_=yq_w[:, cols].bitcast(I32))
+
+        def after(tag, name):
+            return tile(name, [P, UNIT], F32, tag=tag)[:]
+
+        scale(0, 0, ring[0][:])
+        scale(0, 1, ring[1][:])
+        shift(0, 0)
+        scale(0, 2, ring[0][:])
+        shift(0, 1)
+        scale(0, 3, ring[1][:])
+        shift(0, 2)
+        scale(1, 0, ring[0][:, 0:UNIT])
+        shift(0, 3)
+        round_z(0)
+        round_z(1)
+        scale(1, 1, ring[1][:, 0:UNIT])
+        shift(1, 0)
+        scale(1, 2, ring[0][:, 0:UNIT])
+        second(0)
+        shift(1, 1)
+        scale(1, 3, after("zb0", "p13"))
+        second(1)
+        finish(0)
+        shift(1, 2)
+        scale(2, 0, res_of(0)[:, 0, :])
+        shift(1, 3)
+        round_z(2)
+        finish(1)
+        hand_on(0)
+        scale(2, 1, res_of(1)[:, 0, :])
+        second(2)
+        shift(2, 0)
+        scale(2, 2, after("zb2", "p22"))
+        hand_on(1)
+        shift(2, 1)
+        scale(2, 3, after("yb1", "p23"))
+        shift(2, 2)
+        shift(2, 3)
+        round_z(3)
+        finish(2)
+        second(3)
+        hand_on(2)
+        finish(3, last=True)
+        hand_on(3)
+        for q in range(4):
+            nc.scalar.dma_start(out=out_2[0, 4 * q : 4 * q + 4, :].bitcast(I32), in_=yq_s[32 * q : 32 * q + 4, :].bitcast(I32))

@@ -39,6 +39,17 @@ def tile_picked_filmres_silu_po_kernel(
     def deal(dst, src):
         nc.vector.tensor_copy(out=dst.rearrange("p (t m) -> p m t", t=PACK), in_=src.rearrange("p (m t) -> p m t", t=PACK))
 
+    def weave(copy, dst, src):
+        copy(out=dst.rearrange("p (c i) t -> p c t i", i=PACK), in_=src.rearrange("p t (c i) -> p c t i", i=PACK))
+
+    def weave_on(engines, dst, src):
+        n = UNIT // len(engines)
+        for e, copy in enumerate(engines):
+            weave(copy, dst[:, e * n : (e + 1) * n, :], src[:, :, e * n : (e + 1) * n])
+
+    scalar_only = [nc.scalar.copy]
+    both = [nc.scalar.copy, nc.vector.tensor_copy]
+
     with ExitStack() as ctx:
         keep = ctx.enter_context(tc.tile_pool(name="keep", bufs=1))
         psum = ctx.enter_context(tc.psum_pool(name="psum", bufs=1))
@@ -62,25 +73,26 @@ def tile_picked_filmres_silu_po_kernel(
         nc.gpsimd.memset(s1_raw[:].bitcast(I32), 0)
         nc.gpsimd.memset(s2_raw[:].bitcast(I32), 0)
 
+        def load_plane(tiles, dram, t):
+            nc.sync.dma_start(out=tiles[t][:], in_=rows_of(dram)[:, t, :])
+
         nc.sync.dma_start(offs_t[:], offs)
-        nc.sync.dma_start(out=w1_raw[:], in_=words_of(w1_words))
         nc.sync.dma_start(out=xw[:].bitcast(I32)[:, 0 : T // 2], in_=words_of(x_words)[:, 0 : T // 2])
         load_scale_rows(nc.sync, xs, x_scales)
+        nc.sync.dma_start(out=w1_raw[:], in_=words_of(w1_words))
         nc.sync.dma_start(out=xw[:].bitcast(I32)[:, T // 2 : T], in_=words_of(x_words)[:, T // 2 : T])
         load_scale_rows(nc.sync, s1_raw, w1_scales)
         nc.sync.dma_start(task_t[:], task)
+        for first in (0, 2):
+            for tiles, dram in ((gam_t, gam), (bet_t, bet)):
+                for t in (first, first + 1):
+                    load_plane(tiles, dram, t)
         nc.sync.dma_start(out=w2_raw[:], in_=words_of(w2_words))
-        nc.sync.dma_start(out=gam_t[0][:], in_=rows_of(gam)[:, 0, :])
         load_scale_rows(nc.sync, s2_raw, w2_scales)
-        for t in range(PACK):
-            if t + 1 < PACK:
-                nc.sync.dma_start(out=gam_t[t + 1][:], in_=rows_of(gam)[:, t + 1, :])
-            nc.sync.dma_start(out=bet_t[t][:], in_=rows_of(bet)[:, t, :])
         for a in range(2):
             nc.sync.dma_start(out=res_t[a][:], in_=rows_of(res)[:, :, a * HALF : (a + 1) * HALF])
 
         xg_s = tile("xg_s", [P, S], U8)
-        xg_w = [tile("xg_w%d" % a, [P, HALF], U32) for a in range(2)]
         w1 = tile("w1", [P, W], I32)
         w2 = tile("w2", [P, W], I32)
         s1 = tile("s1", [P, W], U8)
@@ -88,12 +100,14 @@ def tile_picked_filmres_silu_po_kernel(
 
         nc.vector.tensor_copy(xg_s[:], xs[:].indirect(offs_t[:]))
         deal(w1[:], w1_raw[:])
+        xg_w = [tile("xg_w0", [P, HALF], U32)]
+        nc.vector.tensor_copy(xg_w[0][:], xw[:].indirect(offs_t[:, 0:16]))
+        deal(s1[:], s1_raw[:])
+        xg_w.append(tile("xg_w1", [P, HALF], U32, tag="s1_raw"))
+        nc.vector.tensor_copy(xg_w[1][:], xw[:].indirect(offs_t[:, 16:32]))
         banks = [psum.tile([P, 512], F32, name="bank%d" % b) for b in range(8)]
         h = [[tile("h%d_%d" % (a, t), [P, HALF], F32) for t in range(PACK)] for a in range(2)]
         for a in range(2):
-            nc.vector.tensor_copy(xg_w[a][:], xw[:].indirect(offs_t[:, 16 * a : 16 * a + 16]))
-            if a == 0:
-                deal(s1[:], s1_raw[:])
             for t in range(PACK):
                 acc = banks[PACK * a + t][:, 0:HALF]
                 nc.tensor.matmul_mx(
@@ -106,35 +120,30 @@ def tile_picked_filmres_silu_po_kernel(
                     stop=True,
                 )
                 nc.scalar.activation(out=h[a][t][:], in_=acc, func=SILU)
-        deal(s2[:], s2_raw[:])
-        deal(w2[:], w2_raw[:])
 
         ring = [tile("ring%d" % i, [P, HALF], F32) for i in range(2)]
-        z = [tile("z0", [P, PACK, HALF], F32), tile("z1", [P, PACK, UNIT], F32), tile("z2", [P, PACK, UNIT], F32)]
-        starts = [0, HALF, HALF + UNIT]
-        widths = [HALF, UNIT, UNIT]
-        zq_w = tile("zq_w", [P, S], U32)
-        zq_s = tile("zq_s", [P, S], U8)
+        z = [tile("z%d" % a, [P, PACK, HALF], F32) for a in range(2)]
         yq_w = tile("yq_w", [P, S], U32)
         yq_s = tile("yq_s", [P, S], U8)
         y = [tile("y%d" % u, [P, PACK, UNIT], F32) for u in range(4)]
         zb, yb, prod = {}, {}, {}
 
-        def lists(c):
-            return task_t[:, starts[c] // 16 : (starts[c] + widths[c]) // 16]
+        def lists(u, n):
+            return task_t[:, u * UNIT // 16 : (u + n) * UNIT // 16]
 
-        def scale(c, t, dst):
-            prod[c, t] = dst
-            a, lo = divmod(starts[c], HALF)
-            nc.vector.tensor_tensor(dst, gam_t[t][:].indirect(lists(c)), h[a][t][:, lo : lo + widths[c]], MULT)
+        def part(u, n):
+            return slice(u % 2 * UNIT, (u % 2 + n) * UNIT)
 
-        def shift(c, t):
-            nc.vector.tensor_tensor(z[c][:, t, :], bet_t[t][:].indirect(lists(c)), prod[c, t], ADD)
+        def scale(u, t, dst, n=1):
+            prod[u, t] = dst[:, 0 : n * UNIT]
+            nc.vector.tensor_tensor(prod[u, t], gam_t[t][:].indirect(lists(u, n)), h[u // 2][t][:, part(u, n)], MULT)
 
-        def round_z(u):
+        def shift(u, t, n=1):
+            nc.vector.tensor_tensor(z[u // 2][:, t, part(u, n)], bet_t[t][:].indirect(lists(u, n)), prod[u, t], ADD)
+
+        def round_z(u, engines=scalar_only):
             zb[u] = tile("zb%d" % u, [P, UNIT, PACK], BF16)
-            src = z[0][:, :, u * UNIT : (u + 1) * UNIT] if u < 2 else z[u - 1][:]
-            nc.scalar.copy(out=zb[u][:], in_=src.rearrange("p t j -> p j t"))
+            weave_on(engines, zb[u], z[u // 2][:, :, part(u, 1)])
 
         def second(u):
             cols = slice(u * UNIT, (u + 1) * UNIT)
@@ -153,15 +162,14 @@ def tile_picked_filmres_silu_po_kernel(
         def res_of(u):
             return res_t[u // 2][:, :, (u % 2) * UNIT : (u % 2 + 1) * UNIT]
 
-        def finish(u, last=False):
+        def finish(u):
             cols = slice(u * UNIT, (u + 1) * UNIT)
             nc.vector.tensor_tensor(y[u][:], banks[u][:].rearrange("p (t j) -> p t j", t=PACK), res_of(u), ADD)
             nc.sync.dma_start(out=rows_of(out_0)[:, :, cols], in_=y[u][:])
+
+        def round_y(u, engines=scalar_only):
             yb[u] = tile("yb%d" % u, [P, UNIT, PACK], BF16)
-            if last:
-                nc.vector.tensor_copy(out=yb[u][:], in_=y[u][:].rearrange("p t j -> p j t"))
-            else:
-                nc.scalar.copy(out=yb[u][:], in_=y[u][:].rearrange("p t j -> p j t"))
+            weave_on(engines, yb[u], y[u])
 
         def hand_on(u):
             cols = slice(u * UNIT, (u + 1) * UNIT)
@@ -169,47 +177,55 @@ def tile_picked_filmres_silu_po_kernel(
             nc.sync.dma_start(out=words_of(out_1)[:, cols], in_=yq_w[:, cols].bitcast(I32))
 
         def after(tag, name):
-            return tile(name, [P, UNIT], F32, tag=tag)[:]
+            return tile(name, [P, 2, UNIT], F32, tag=tag)
 
-        scale(0, 0, ring[0][:])
-        scale(0, 1, ring[1][:])
-        shift(0, 0)
-        scale(0, 2, ring[0][:])
-        shift(0, 1)
-        scale(0, 3, ring[1][:])
-        shift(0, 2)
-        scale(1, 0, ring[0][:, 0:UNIT])
-        shift(0, 3)
+        for first in (0, 2):
+            for t in (first, first + 1):
+                scale(0, t, ring[t % 2], n=2)
+            for t in (first, first + 1):
+                shift(0, t, n=2)
         round_z(0)
         round_z(1)
-        scale(1, 1, ring[1][:, 0:UNIT])
-        shift(1, 0)
-        scale(1, 2, ring[0][:, 0:UNIT])
+        deal(w2[:], w2_raw[:])
+        deal(s2[:], s2_raw[:])
+        zq_w = tile("zq_w", [P, S], U32, tag="w2_raw")
+        zq_s = tile("zq_s", [P, S], U8, tag="s2_raw")
         second(0)
-        shift(1, 1)
-        scale(1, 3, after("zb0", "p13"))
+        pair = after("zb0", "p20")
+        scale(2, 0, pair[:, 0, :])
+        scale(2, 1, pair[:, 1, :])
         second(1)
-        finish(0)
-        shift(1, 2)
-        scale(2, 0, res_of(0)[:, 0, :])
-        shift(1, 3)
-        round_z(2)
-        finish(1)
-        hand_on(0)
-        scale(2, 1, res_of(1)[:, 0, :])
-        second(2)
         shift(2, 0)
-        scale(2, 2, after("zb2", "p22"))
-        hand_on(1)
+        finish(0)
+        round_y(0)
         shift(2, 1)
-        scale(2, 3, after("yb1", "p23"))
+        finish(1)
+        round_y(1)
+        scale(2, 2, res_of(1)[:, 0, :])
+        scale(2, 3, res_of(1)[:, 1, :])
+        hand_on(0)
         shift(2, 2)
         shift(2, 3)
-        round_z(3)
-        finish(2)
+        round_z(2)
+        pair = after("yb0", "p30")
+        scale(3, 0, pair[:, 0, :])
+        scale(3, 1, pair[:, 1, :])
+        second(2)
+        shift(3, 0)
+        shift(3, 1)
+        pair = after("zb2", "p32")
+        scale(3, 2, pair[:, 0, :])
+        scale(3, 3, pair[:, 1, :])
+        shift(3, 2)
+        shift(3, 3)
+        round_z(3, both)
+        hand_on(1)
         second(3)
+        finish(2)
+        round_y(2)
+        finish(3)
         hand_on(2)
-        finish(3, last=True)
+        round_y(3, both)
         hand_on(3)
         for q in range(4):
             nc.scalar.dma_start(out=out_2[0, 4 * q : 4 * q + 4, :].bitcast(I32), in_=yq_s[32 * q : 32 * q + 4, :].bitcast(I32))

@@ -135,11 +135,11 @@ def tile_picked_filmres_silu_po_kernel(
             return slice(u % 2 * UNIT, (u % 2 + n) * UNIT)
 
         def scale(u, t, dst, n=1):
-            prod[u, t] = dst[:, 0 : n * UNIT]
-            nc.vector.tensor_tensor(prod[u, t], gam_t[t][:].indirect(lists(u, n)), h[u // 2][t][:, part(u, n)], MULT)
+            prod[u // 2, t] = dst
+            nc.vector.tensor_tensor(dst, gam_t[t][:].indirect(lists(u, n)), h[u // 2][t][:, part(u, n)], MULT)
 
         def shift(u, t, n=1):
-            nc.vector.tensor_tensor(z[u // 2][:, t, part(u, n)], bet_t[t][:].indirect(lists(u, n)), prod[u, t], ADD)
+            nc.vector.tensor_tensor(z[u // 2][:, t, part(u, n)], bet_t[t][:].indirect(lists(u, n)), prod[u // 2, t][:, part(u, n)], ADD)
 
         def round_z(u, engines=scalar_only):
             zb[u] = tile("zb%d" % u, [P, UNIT, PACK], BF16)
@@ -181,7 +181,7 @@ def tile_picked_filmres_silu_po_kernel(
 
         for first in (0, 2):
             for t in (first, first + 1):
-                scale(0, t, ring[t % 2], n=2)
+                scale(0, t, ring[t % 2][:], n=2)
             for t in (first, first + 1):
                 shift(0, t, n=2)
         round_z(0)
@@ -191,41 +191,33 @@ def tile_picked_filmres_silu_po_kernel(
         zq_w = tile("zq_w", [P, S], U32, tag="w2_raw")
         zq_s = tile("zq_s", [P, S], U8, tag="s2_raw")
         second(0)
-        pair = after("zb0", "p20")
-        scale(2, 0, pair[:, 0, :])
-        scale(2, 1, pair[:, 1, :])
+        pair = tile("pair", [P, 2, HALF], F32, tag="zb0")
+        scale(2, 0, pair[:, 0, :], n=2)
+        scale(2, 1, pair[:, 1, :], n=2)
         second(1)
-        shift(2, 0)
+        shift(2, 0, n=2)
         finish(0)
         round_y(0)
-        shift(2, 1)
+        shift(2, 1, n=2)
         finish(1)
         round_y(1)
-        scale(2, 2, res_of(1)[:, 0, :])
-        scale(2, 3, res_of(1)[:, 1, :])
+        scale(2, 2, res_t[0][:, 0, :], n=2)
+        scale(2, 3, res_t[0][:, 1, :], n=2)
         hand_on(0)
         shift(2, 2)
         shift(2, 3)
         round_z(2)
-        pair = after("yb0", "p30")
-        scale(3, 0, pair[:, 0, :])
-        scale(3, 1, pair[:, 1, :])
-        second(2)
-        shift(3, 0)
-        shift(3, 1)
-        pair = after("zb2", "p32")
-        scale(3, 2, pair[:, 0, :])
-        scale(3, 3, pair[:, 1, :])
+        hand_on(1)
         shift(3, 2)
         shift(3, 3)
         round_z(3, both)
-        hand_on(1)
+        second(2)
         second(3)
         finish(2)
         round_y(2)
         finish(3)
-        hand_on(2)
         round_y(3, both)
+        hand_on(2)
         hand_on(3)
         for q in range(4):
-            nc.scalar.dma_start(out=out_2[0, 4 * q : 4 * q + 4, :].bitcast(I32), in_=yq_s[32 * q : 32 * q + 4, :].bitcast(I32))
+            (nc.sync if q == 0 else nc.scalar).dma_start(out=out_2[0, 4 * q : 4 * q + 4, :].bitcast(I32), in_=yq_s[32 * q : 32 * q + 4, :].bitcast(I32))

@@ -15,8 +15,11 @@ SILU = mybir.ActivationFunctionType.Silu
 
 P = 128
 PACK = 4
-T, S, W = 2048, 512, 512
-HALF = 256
+QUADS = 4
+TOKENS = 2048
+S = 512
+W = 512
+HALF = S // 2
 UNIT = 128
 FLOPS = 2 * 2 * 512 * 512 * 512
 
@@ -29,195 +32,162 @@ def tile_picked_filmres_silu_po_kernel(
     def words_of(dram):
         return dram[0].rearrange("p n t -> p (n t)").bitcast(I32)
 
-    def rows_of(dram):
+    def planes_of(dram):
         return dram.rearrange("(p t) c -> p t c", t=PACK)
 
-    def load_scale_rows(queue, plane, dram):
-        for q in range(4):
-            queue.dma_start(out=plane[32 * q : 32 * q + 4, :].bitcast(I32), in_=dram[0, 4 * q : 4 * q + 4, :].bitcast(I32))
+    def scale_rows(plane, dram, q):
+        return plane[32 * q : 32 * q + 4, :].bitcast(I32), dram[0, 4 * q : 4 * q + 4, :].bitcast(I32)
+
+    def load_scales(plane, dram):
+        for q in range(QUADS):
+            rows, source = scale_rows(plane, dram, q)
+            nc.sync.dma_start(out=rows, in_=source)
 
     def deal(dst, src):
         nc.vector.tensor_copy(out=dst.rearrange("p (t m) -> p m t", t=PACK), in_=src.rearrange("p (m t) -> p m t", t=PACK))
 
     def weave(copy, dst, src):
-        copy(out=dst.rearrange("p (c i) t -> p c t i", i=PACK), in_=src.rearrange("p t (c i) -> p c t i", i=PACK))
+        copy(out=dst.rearrange("p (c i) t -> p c t i", i=4), in_=src.rearrange("p t (c i) -> p c t i", i=4))
 
-    def weave_on(engines, dst, src):
-        n = UNIT // len(engines)
-        for e, copy in enumerate(engines):
-            weave(copy, dst[:, e * n : (e + 1) * n, :], src[:, :, e * n : (e + 1) * n])
+    def product(acc, weights, weight_scales, t, codes, scales):
+        rows = slice(t * P, (t + 1) * P)
+        nc.tensor.matmul_mx(
+            out=acc,
+            lhsT=weights[:, rows].bitcast(FP8X4),
+            lhsT_scale=weight_scales[:, rows],
+            rhs=codes.bitcast(FP8X4),
+            rhs_scale=scales,
+            start=True,
+            stop=True,
+        )
 
-    scalar_only = [nc.scalar.copy]
-    both = [nc.scalar.copy, nc.vector.tensor_copy]
+    def quantise(codes, scales, woven):
+        nc.vector.quantize_mx(out=codes.bitcast(FP8X4), scales=scales, in_=woven.rearrange("p c t -> p (c t)"))
 
     with ExitStack() as ctx:
         keep = ctx.enter_context(tc.tile_pool(name="keep", bufs=1))
         psum = ctx.enter_context(tc.psum_pool(name="psum", bufs=1))
 
-        def tile(name, shape, dtype, tag=None):
-            return keep.tile(shape, dtype, name=name, tag=tag or name, align_bytes=64)
+        def tile(name, shape, dtype):
+            return keep.tile(shape, dtype, name=name, align_bytes=64)
 
         offs_t = tile("offs_t", [P, S // 16], U16)
         task_t = tile("task_t", [P, S // 16], U16)
-        xw = tile("xw", [P, T], U32)
-        xs = tile("xs", [P, T], U8)
+        x_w = tile("x_w", [P, TOKENS], U32)
+        x_s = tile("x_s", [P, TOKENS], U8)
         w1_raw = tile("w1_raw", [P, W], I32)
         w2_raw = tile("w2_raw", [P, W], I32)
         s1_raw = tile("s1_raw", [P, W], U8)
         s2_raw = tile("s2_raw", [P, W], U8)
-        gam_t = [tile("gam%d" % t, [P, W], F32) for t in range(PACK)]
-        bet_t = [tile("bet%d" % t, [P, W], F32) for t in range(PACK)]
-        res_t = [tile("res%d" % a, [P, PACK, HALF], F32) for a in range(2)]
+        res_t = tile("res_t", [P, PACK, S], F32)
+        last = PACK - 1
+        gam_t = [tile("gam%d" % t, [P, 2 * W], F32) for t in range(PACK)]
+        bet_t = [tile("bet%d" % t, [P, W if t == last else 2 * W], F32) for t in range(PACK)]
 
-        nc.vector.memset(xs[:].bitcast(I32), 0)
+        nc.vector.memset(x_s[:].bitcast(I32), 0)
         nc.gpsimd.memset(s1_raw[:].bitcast(I32), 0)
         nc.gpsimd.memset(s2_raw[:].bitcast(I32), 0)
 
         def load_plane(tiles, dram, t):
-            nc.sync.dma_start(out=tiles[t][:], in_=rows_of(dram)[:, t, :])
+            nc.sync.dma_start(out=tiles[t][:, 0:W], in_=planes_of(dram)[:, t, :])
+
+        def load_x_half(a):
+            cols = slice(a * TOKENS // 2, (a + 1) * TOKENS // 2)
+            nc.sync.dma_start(out=x_w[:].bitcast(I32)[:, cols], in_=words_of(x_words)[:, cols])
 
         nc.sync.dma_start(offs_t[:], offs)
-        nc.sync.dma_start(out=xw[:].bitcast(I32)[:, 0 : T // 2], in_=words_of(x_words)[:, 0 : T // 2])
-        load_scale_rows(nc.sync, xs, x_scales)
+        load_x_half(0)
+        load_scales(x_s, x_scales)
         nc.sync.dma_start(out=w1_raw[:], in_=words_of(w1_words))
-        nc.sync.dma_start(out=xw[:].bitcast(I32)[:, T // 2 : T], in_=words_of(x_words)[:, T // 2 : T])
-        load_scale_rows(nc.sync, s1_raw, w1_scales)
+        load_x_half(1)
+        load_scales(s1_raw, w1_scales)
         nc.sync.dma_start(task_t[:], task)
-        for first in (0, 2):
-            for tiles, dram in ((gam_t, gam), (bet_t, bet)):
-                for t in (first, first + 1):
-                    load_plane(tiles, dram, t)
+        for tiles, dram, t in (
+            (bet_t, bet, 0), (gam_t, gam, 0), (gam_t, gam, 1), (bet_t, bet, 1),
+            (gam_t, gam, 2), (gam_t, gam, 3), (bet_t, bet, 2), (bet_t, bet, 3),
+        ):
+            load_plane(tiles, dram, t)
         nc.sync.dma_start(out=w2_raw[:], in_=words_of(w2_words))
-        load_scale_rows(nc.sync, s2_raw, w2_scales)
-        for a in range(2):
-            nc.sync.dma_start(out=res_t[a][:], in_=rows_of(res)[:, :, a * HALF : (a + 1) * HALF])
+        load_scales(s2_raw, w2_scales)
+        nc.sync.dma_start(out=res_t[:], in_=planes_of(res))
 
-        xg_s = tile("xg_s", [P, S], U8)
-        w1 = tile("w1", [P, W], I32)
-        w2 = tile("w2", [P, W], I32)
-        s1 = tile("s1", [P, W], U8)
-        s2 = tile("s2", [P, W], U8)
-
-        nc.vector.tensor_copy(xg_s[:], xs[:].indirect(offs_t[:]))
+        picked_s = tile("picked_s", [P, S], U8)
+        picked_w = tile("picked_w", [P, S], U32)
+        w1, s1 = tile("w1", [P, W], I32), tile("s1", [P, W], U8)
+        nc.vector.tensor_copy(picked_s[:], x_s[:].indirect(offs_t[:]))
         deal(w1[:], w1_raw[:])
-        xg_w = [tile("xg_w0", [P, HALF], U32)]
-        nc.vector.tensor_copy(xg_w[0][:], xw[:].indirect(offs_t[:, 0:16]))
+        nc.vector.tensor_copy(picked_w[:], x_w[:].indirect(offs_t[:]))
         deal(s1[:], s1_raw[:])
-        xg_w.append(tile("xg_w1", [P, HALF], U32, tag="s1_raw"))
-        nc.vector.tensor_copy(xg_w[1][:], xw[:].indirect(offs_t[:, 16:32]))
-        banks = [psum.tile([P, 512], F32, name="bank%d" % b) for b in range(8)]
-        h = [[tile("h%d_%d" % (a, t), [P, HALF], F32) for t in range(PACK)] for a in range(2)]
-        for a in range(2):
-            for t in range(PACK):
-                acc = banks[PACK * a + t][:, 0:HALF]
-                nc.tensor.matmul_mx(
-                    out=acc,
-                    lhsT=w1[:, t * P : (t + 1) * P].bitcast(FP8X4),
-                    lhsT_scale=s1[:, t * P : (t + 1) * P],
-                    rhs=xg_w[a][:].bitcast(FP8X4),
-                    rhs_scale=xg_s[:, a * HALF : (a + 1) * HALF],
-                    start=True,
-                    stop=True,
-                )
-                nc.scalar.activation(out=h[a][t][:], in_=acc, func=SILU)
+        h = [tile("h%d" % t, [P, S], F32) for t in range(PACK)]
+        for t in range(PACK):
+            first_acc = psum.tile([P, S], F32, name="first_acc%d" % t)
+            product(first_acc[:], w1, s1, t, picked_w[:], picked_s[:])
+            nc.scalar.activation(out=h[t][:], in_=first_acc[:], func=SILU)
 
-        ring = [tile("ring%d" % i, [P, HALF], F32) for i in range(2)]
-        z = [tile("z%d" % a, [P, PACK, HALF], F32) for a in range(2)]
-        yq_w = tile("yq_w", [P, S], U32)
-        yq_s = tile("yq_s", [P, S], U8)
-        y = [tile("y%d" % u, [P, PACK, UNIT], F32) for u in range(4)]
-        zb, yb, prod = {}, {}, {}
+        z = tile("z", [P, PACK, S], F32)
+        scaled = [tile("scaled%d" % i, [P, S], F32) for i in range(2)]
+        shift0 = tile("shift0", [P, S], F32)
 
-        def lists(u, n):
-            return task_t[:, u * UNIT // 16 : (u + n) * UNIT // 16]
+        def scale(t):
+            nc.vector.tensor_tensor(scaled[t % 2][:], gam_t[t][:].indirect(task_t[:]), h[t][:], MULT)
 
-        def part(u, n):
-            return slice(u % 2 * UNIT, (u % 2 + n) * UNIT)
+        def shift(t, lo, hi):
+            lists = task_t[:, lo // 16 : hi // 16]
+            nc.vector.tensor_tensor(z[:, t, lo:hi], bet_t[t][:].indirect(lists), scaled[t % 2][:, lo:hi], ADD)
 
-        def scale(u, t, dst, n=1):
-            prod[u // 2, t] = dst
-            nc.vector.tensor_tensor(dst, gam_t[t][:].indirect(lists(u, n)), h[u // 2][t][:, part(u, n)], MULT)
+        nc.vector.tensor_copy(shift0[:], bet_t[0][:].indirect(task_t[:]))
+        scale(0)
+        scale(1)
+        nc.vector.tensor_tensor(z[:, 0, :], shift0[:], scaled[0][:], ADD)
+        shift(1, 0, S)
+        scale(2)
+        scale(3)
+        shift(2, 0, S)
+        shift(last, 0, HALF)
+        shift(last, HALF, S)
 
-        def shift(u, t, n=1):
-            nc.vector.tensor_tensor(z[u // 2][:, t, part(u, n)], bet_t[t][:].indirect(lists(u, n)), prod[u // 2, t][:, part(u, n)], ADD)
-
-        def round_z(u, engines=scalar_only):
-            zb[u] = tile("zb%d" % u, [P, UNIT, PACK], BF16)
-            weave_on(engines, zb[u], z[u // 2][:, :, part(u, 1)])
-
-        def second(u):
-            cols = slice(u * UNIT, (u + 1) * UNIT)
-            nc.vector.quantize_mx(out=zq_w[:, cols].bitcast(FP8X4), scales=zq_s[:, cols], in_=zb[u][:].rearrange("p j t -> p (j t)"))
-            for t in range(PACK):
-                nc.tensor.matmul_mx(
-                    out=banks[u][:, t * UNIT : (t + 1) * UNIT],
-                    lhsT=w2[:, t * P : (t + 1) * P].bitcast(FP8X4),
-                    lhsT_scale=s2[:, t * P : (t + 1) * P],
-                    rhs=zq_w[:, cols].bitcast(FP8X4),
-                    rhs_scale=zq_s[:, cols],
-                    start=True,
-                    stop=True,
-                )
-
-        def res_of(u):
-            return res_t[u // 2][:, :, (u % 2) * UNIT : (u % 2 + 1) * UNIT]
-
-        def finish(u):
-            cols = slice(u * UNIT, (u + 1) * UNIT)
-            nc.vector.tensor_tensor(y[u][:], banks[u][:].rearrange("p (t j) -> p t j", t=PACK), res_of(u), ADD)
-            nc.sync.dma_start(out=rows_of(out_0)[:, :, cols], in_=y[u][:])
-
-        def round_y(u, engines=scalar_only):
-            yb[u] = tile("yb%d" % u, [P, UNIT, PACK], BF16)
-            weave_on(engines, yb[u], y[u])
-
-        def hand_on(u):
-            cols = slice(u * UNIT, (u + 1) * UNIT)
-            nc.vector.quantize_mx(out=yq_w[:, cols].bitcast(FP8X4), scales=yq_s[:, cols], in_=yb[u][:].rearrange("p j t -> p (j t)"))
-            nc.sync.dma_start(out=words_of(out_1)[:, cols], in_=yq_w[:, cols].bitcast(I32))
-
-        def after(tag, name):
-            return tile(name, [P, 2, UNIT], F32, tag=tag)
-
-        for first in (0, 2):
-            for t in (first, first + 1):
-                scale(0, t, ring[t % 2][:], n=2)
-            for t in (first, first + 1):
-                shift(0, t, n=2)
-        round_z(0)
-        round_z(1)
+        w2, s2 = tile("w2", [P, W], I32), tile("s2", [P, W], U8)
         deal(w2[:], w2_raw[:])
         deal(s2[:], s2_raw[:])
-        zq_w = tile("zq_w", [P, S], U32, tag="w2_raw")
-        zq_s = tile("zq_s", [P, S], U8, tag="s2_raw")
-        second(0)
-        pair = tile("pair", [P, 2, HALF], F32, tag="zb0")
-        scale(2, 0, pair[:, 0, :], n=2)
-        scale(2, 1, pair[:, 1, :], n=2)
-        second(1)
-        shift(2, 0, n=2)
-        finish(0)
-        round_y(0)
-        shift(2, 1, n=2)
-        finish(1)
-        round_y(1)
-        scale(2, 2, res_t[0][:, 0, :], n=2)
-        scale(2, 3, res_t[0][:, 1, :], n=2)
-        hand_on(0)
-        shift(2, 2)
-        shift(2, 3)
-        round_z(2)
-        hand_on(1)
-        shift(3, 2)
-        shift(3, 3)
-        round_z(3, both)
-        second(2)
-        second(3)
-        finish(2)
-        round_y(2)
-        finish(3)
-        round_y(3, both)
-        hand_on(2)
-        hand_on(3)
-        for q in range(4):
-            (nc.sync if q == 0 else nc.scalar).dma_start(out=out_2[0, 4 * q : 4 * q + 4, :].bitcast(I32), in_=yq_s[32 * q : 32 * q + 4, :].bitcast(I32))
+
+        units = S // UNIT
+        z_w, z_s = tile("z_w", [P, S], U32), tile("z_s", [P, S], U8)
+        y_w, y_s = tile("y_w", [P, S], U32), tile("y_s", [P, S], U8)
+        y_woven = tile("y_woven", [P, S, PACK], BF16)
+        second_acc = [psum.tile([P, PACK, UNIT], F32, name="second_acc%d" % u) for u in range(units)]
+
+        def multiply(u):
+            cols = slice(u * UNIT, (u + 1) * UNIT)
+            z_woven = tile("z_woven%d" % u, [P, UNIT, PACK], BF16)
+            weave(nc.scalar.copy, z_woven[:], z[:, :, cols])
+            quantise(z_w[:, cols], z_s[:, cols], z_woven[:])
+            for t in range(PACK):
+                product(second_acc[u][:, t, :], w2, s2, t, z_w[:, cols], z_s[:, cols])
+
+        def add_residual(u):
+            cols = slice(u * UNIT, (u + 1) * UNIT)
+            y = tile("y%d" % u, [P, PACK, UNIT], F32)
+            nc.vector.tensor_tensor(y[:], second_acc[u][:], res_t[:, :, cols], ADD)
+            nc.sync.dma_start(out=planes_of(out_0)[:, :, cols], in_=y[:])
+            copies = [nc.scalar.copy, nc.vector.tensor_copy] if u == units - 1 else [nc.scalar.copy]
+            share = UNIT // len(copies)
+            for e, copy in enumerate(copies):
+                lo = u * UNIT + e * share
+                weave(copy, y_woven[:, lo : lo + share, :], y[:, :, e * share : (e + 1) * share])
+
+        def hand_on(lo, hi):
+            cols = slice(lo, hi)
+            quantise(y_w[:, cols], y_s[:, cols], y_woven[:, cols, :])
+            nc.sync.dma_start(out=words_of(out_1)[:, cols], in_=y_w[:, cols].bitcast(I32))
+
+        multiply(0)
+        for u in range(units):
+            if u + 1 < units:
+                multiply(u + 1)
+            add_residual(u)
+        hand_on(0, HALF)
+        hand_on(HALF, S - UNIT)
+        hand_on(S - UNIT, S)
+        for q in range(QUADS):
+            rows, target = scale_rows(y_s, out_2, q)
+            (nc.sync if q == 0 else nc.scalar).dma_start(out=target, in_=rows)

@@ -35,16 +35,18 @@ def tile_picked_filmres_silu_po_kernel(
     def planes_of(dram):
         return dram.rearrange("(p t) c -> p t c", t=PACK)
 
-    def scale_rows(plane, dram, q):
-        return plane[32 * q : 32 * q + 4, :].bitcast(I32), dram[0, 4 * q : 4 * q + 4, :].bitcast(I32)
+    def scale_rows(plane, dram, r):
+        return plane[r:P:32, :].bitcast(I32), dram[0, r : 4 * QUADS : 4, :].bitcast(I32)
 
-    def load_scales(plane, dram):
-        for q in range(QUADS):
-            rows, source = scale_rows(plane, dram, q)
-            nc.sync.dma_start(out=rows, in_=source)
+    def load_scales(plane, dram, queue=nc.sync):
+        for r in range(4):
+            rows, source = scale_rows(plane, dram, r)
+            queue.dma_start(out=rows, in_=source)
 
-    def deal(dst, src):
-        nc.vector.tensor_copy(out=dst.rearrange("p (t m) -> p m t", t=PACK), in_=src.rearrange("p (m t) -> p m t", t=PACK))
+    def deal(dst, src, lo=0, hi=PACK):
+        nc.vector.tensor_copy(
+            out=dst.rearrange("p (t m) -> p m t", t=PACK)[:, :, lo:hi], in_=src.rearrange("p (m t) -> p m t", t=PACK)[:, :, lo:hi]
+        )
 
     def weave(copy, dst, src):
         copy(out=dst.rearrange("p (c i) t -> p c t i", i=4), in_=src.rearrange("p t (c i) -> p c t i", i=4))
@@ -80,9 +82,8 @@ def tile_picked_filmres_silu_po_kernel(
         s1_raw = tile("s1_raw", [P, W], U8)
         s2_raw = tile("s2_raw", [P, W], U8)
         res_t = tile("res_t", [P, PACK, S], F32)
-        last = PACK - 1
         gam_t = [tile("gam%d" % t, [P, 2 * W], F32) for t in range(PACK)]
-        bet_t = [tile("bet%d" % t, [P, W if t == last else 2 * W], F32) for t in range(PACK)]
+        bet_t = [tile("bet%d" % t, [P, W if t >= 2 else 2 * W], F32) for t in range(PACK)]
 
         nc.vector.memset(x_s[:].bitcast(I32), 0)
         nc.gpsimd.memset(s1_raw[:].bitcast(I32), 0)
@@ -98,71 +99,88 @@ def tile_picked_filmres_silu_po_kernel(
         nc.sync.dma_start(offs_t[:], offs)
         load_x_half(0)
         load_scales(x_s, x_scales)
-        nc.sync.dma_start(out=w1_raw[:], in_=words_of(w1_words))
         load_x_half(1)
+        nc.sync.dma_start(out=w1_raw[:], in_=words_of(w1_words))
         load_scales(s1_raw, w1_scales)
         nc.sync.dma_start(task_t[:], task)
+        load_plane(bet_t, bet, 0)
+        nc.sync.dma_start(out=w2_raw[:], in_=words_of(w2_words))
+        load_plane(gam_t, gam, 0)
+        load_plane(gam_t, gam, 1)
+        load_scales(s2_raw, w2_scales)
         for tiles, dram, t in (
-            (bet_t, bet, 0), (gam_t, gam, 0), (gam_t, gam, 1), (bet_t, bet, 1),
-            (gam_t, gam, 2), (gam_t, gam, 3), (bet_t, bet, 2), (bet_t, bet, 3),
+            (bet_t, bet, 1),
+            (gam_t, gam, 2), (gam_t, gam, 3),
         ):
             load_plane(tiles, dram, t)
-        nc.sync.dma_start(out=w2_raw[:], in_=words_of(w2_words))
-        load_scales(s2_raw, w2_scales)
         nc.sync.dma_start(out=res_t[:], in_=planes_of(res))
+        load_plane(bet_t, bet, 2)
+        load_plane(bet_t, bet, 3)
 
         picked_s = tile("picked_s", [P, S], U8)
         picked_w = tile("picked_w", [P, S], U32)
-        w1, s1 = tile("w1", [P, W], I32), tile("s1", [P, W], U8)
-        nc.vector.tensor_copy(picked_s[:], x_s[:].indirect(offs_t[:]))
-        deal(w1[:], w1_raw[:])
-        nc.vector.tensor_copy(picked_w[:], x_w[:].indirect(offs_t[:]))
-        deal(s1[:], s1_raw[:])
-        h = [tile("h%d" % t, [P, S], F32) for t in range(PACK)]
-        for t in range(PACK):
-            first_acc = psum.tile([P, S], F32, name="first_acc%d" % t)
-            product(first_acc[:], w1, s1, t, picked_w[:], picked_s[:])
-            nc.scalar.activation(out=h[t][:], in_=first_acc[:], func=SILU)
-
-        z = tile("z", [P, PACK, S], F32)
-        scaled = [tile("scaled%d" % i, [P, S], F32) for i in range(2)]
         shift0 = tile("shift0", [P, S], F32)
+        w1, s1 = tile("w1", [P, W], I32), tile("s1", [P, W], U8)
+        w2, s2 = tile("w2", [P, W], I32), tile("s2", [P, W], U8)
+        nc.vector.tensor_copy(picked_s[:], x_s[:].indirect(offs_t[:]))
+        nc.vector.tensor_copy(picked_w[:], x_w[:].indirect(offs_t[:]))
+        deal(w1[:], w1_raw[:])
+        deal(s1[:], s1_raw[:], 0, 1)
+        deal(s1[:], s1_raw[:], 1, PACK)
+        nc.vector.tensor_copy(shift0[:], bet_t[0][:].indirect(task_t[:]))
+        deal(w2[:], w2_raw[:])
+        h = [tile("h%d" % t, [P, S], F32) for t in range(PACK)]
+        for bank, (t, lo, hi) in enumerate([(0, 0, HALF), (0, HALF, S), (1, 0, S), (2, 0, S), (3, 0, S)]):
+            first_acc = psum.tile([P, hi - lo], F32, name="first_acc%d" % bank, tag="bank%d" % bank)
+            product(first_acc[:], w1, s1, t, picked_w[:, lo:hi], picked_s[:, lo:hi])
+            nc.scalar.activation(out=h[t][:, lo:hi], in_=first_acc[:], func=SILU)
+
+        units = S // UNIT
+        z_low = tile("z_low", [P, 2, S], F32)
+        z_high = [tile("z_high%d" % a, [P, 2 * HALF], F32) for a in range(2)]
+        scaled = [tile("scaled%d" % i, [P, S], F32) for i in range(2)]
+        z_woven = [tile("z_woven%d" % u, [P, UNIT, PACK], BF16)[:] for u in range(units)]
 
         def scale(t):
             nc.vector.tensor_tensor(scaled[t % 2][:], gam_t[t][:].indirect(task_t[:]), h[t][:], MULT)
 
-        def shift(t, lo, hi):
+        def shift(out, t, lo, hi):
             lists = task_t[:, lo // 16 : hi // 16]
-            nc.vector.tensor_tensor(z[:, t, lo:hi], bet_t[t][:].indirect(lists), scaled[t % 2][:, lo:hi], ADD)
+            nc.vector.tensor_tensor(out, bet_t[t][:].indirect(lists), scaled[t % 2][:, lo:hi], ADD)
 
-        nc.vector.tensor_copy(shift0[:], bet_t[0][:].indirect(task_t[:]))
-        scale(0)
-        scale(1)
-        nc.vector.tensor_tensor(z[:, 0, :], shift0[:], scaled[0][:], ADD)
-        shift(1, 0, S)
-        scale(2)
-        scale(3)
-        shift(2, 0, S)
-        shift(last, 0, HALF)
-        shift(last, HALF, S)
+        def shift_high(t, a):
+            shift(z_high[a][:, (t - 2) * HALF : (t - 1) * HALF], t, a * HALF, (a + 1) * HALF)
 
-        w2, s2 = tile("w2", [P, W], I32), tile("s2", [P, W], U8)
-        deal(w2[:], w2_raw[:])
-        deal(s2[:], s2_raw[:])
+        def weave_pair(u, pair, src):
+            nc.scalar.copy(out=z_woven[u][:, :, 2 * pair : 2 * pair + 2], in_=src.rearrange("p t c -> p c t"))
 
-        units = S // UNIT
         z_w, z_s = tile("z_w", [P, S], U32), tile("z_s", [P, S], U8)
         y_w, y_s = tile("y_w", [P, S], U32), tile("y_s", [P, S], U8)
         y_woven = tile("y_woven", [P, S, PACK], BF16)
-        second_acc = [psum.tile([P, PACK, UNIT], F32, name="second_acc%d" % u) for u in range(units)]
+        second_acc = [psum.tile([P, PACK, UNIT], F32, name="second_acc%d" % u, tag="bank%d" % u) for u in range(units)]
 
         def multiply(u):
             cols = slice(u * UNIT, (u + 1) * UNIT)
-            z_woven = tile("z_woven%d" % u, [P, UNIT, PACK], BF16)
-            weave(nc.scalar.copy, z_woven[:], z[:, :, cols])
-            quantise(z_w[:, cols], z_s[:, cols], z_woven[:])
+            inner = (u % 2) * UNIT
+            weave_pair(u, 1, z_high[u // 2][:].rearrange("p (t c) -> p t c", t=2)[:, :, inner : inner + UNIT])
+            quantise(z_w[:, cols], z_s[:, cols], z_woven[u])
             for t in range(PACK):
                 product(second_acc[u][:, t, :], w2, s2, t, z_w[:, cols], z_s[:, cols])
+
+        scale(0)
+        scale(1)
+        nc.vector.tensor_tensor(z_low[:, 0, :], shift0[:], scaled[0][:], ADD)
+        shift(z_low[:, 1, :], 1, 0, S)
+        for u in range(units):
+            weave_pair(u, 0, z_low[:, :, u * UNIT : (u + 1) * UNIT])
+        deal(s2[:], s2_raw[:])
+        scale(2)
+        scale(3)
+        shift_high(2, 0)
+        shift_high(3, 0)
+        shift_high(2, 1)
+        shift_high(3, 1)
+        multiply(0)
 
         def add_residual(u):
             cols = slice(u * UNIT, (u + 1) * UNIT)
@@ -180,7 +198,6 @@ def tile_picked_filmres_silu_po_kernel(
             quantise(y_w[:, cols], y_s[:, cols], y_woven[:, cols, :])
             nc.sync.dma_start(out=words_of(out_1)[:, cols], in_=y_w[:, cols].bitcast(I32))
 
-        multiply(0)
         for u in range(units):
             if u + 1 < units:
                 multiply(u + 1)

@@ -1,6 +1,7 @@
 from contextlib import ExitStack
 
 import concourse.mybir as mybir
+from concourse.masks import make_identity
 
 F32 = mybir.dt.float32
 BF16 = mybir.dt.bfloat16
@@ -89,6 +90,9 @@ def tile_picked_filmres_silu_po_kernel(
         nc.gpsimd.memset(s1_raw[:].bitcast(I32), 0)
         nc.gpsimd.memset(s2_raw[:].bitcast(I32), 0)
 
+        identity = tile("identity", [P, P], F32)
+        make_identity(nc, identity[:])
+
         def load_plane(tiles, dram, t):
             nc.sync.dma_start(out=tiles[t][:, 0:W], in_=planes_of(dram)[:, t, :])
 
@@ -108,14 +112,9 @@ def tile_picked_filmres_silu_po_kernel(
         load_plane(gam_t, gam, 0)
         load_plane(gam_t, gam, 1)
         load_scales(s2_raw, w2_scales)
-        for tiles, dram, t in (
-            (bet_t, bet, 1),
-            (gam_t, gam, 2), (gam_t, gam, 3),
-        ):
+        for tiles, dram, t in ((gam_t, gam, 2), (bet_t, bet, 1), (gam_t, gam, 3), (bet_t, bet, 2), (bet_t, bet, 3)):
             load_plane(tiles, dram, t)
         nc.sync.dma_start(out=res_t[:], in_=planes_of(res))
-        load_plane(bet_t, bet, 2)
-        load_plane(bet_t, bet, 3)
 
         picked_s = tile("picked_s", [P, S], U8)
         picked_w = tile("picked_w", [P, S], U32)
@@ -138,15 +137,15 @@ def tile_picked_filmres_silu_po_kernel(
         units = S // UNIT
         z_low = tile("z_low", [P, 2, S], F32)
         z_high = [tile("z_high%d" % a, [P, 2 * HALF], F32) for a in range(2)]
-        scaled = [tile("scaled%d" % i, [P, S], F32) for i in range(2)]
-        z_woven = [tile("z_woven%d" % u, [P, UNIT, PACK], BF16)[:] for u in range(units)]
+        scaled = [tile("scaled%d" % i, [P, S], F32) for i in range(PACK)]
+        z_woven = [tile("z_woven%d" % u, [P, UNIT, PACK], BF16) for u in range(units)]
 
         def scale(t):
-            nc.vector.tensor_tensor(scaled[t % 2][:], gam_t[t][:].indirect(task_t[:]), h[t][:], MULT)
+            nc.vector.tensor_tensor(scaled[t][:], gam_t[t][:].indirect(task_t[:]), h[t][:], MULT)
 
         def shift(out, t, lo, hi):
             lists = task_t[:, lo // 16 : hi // 16]
-            nc.vector.tensor_tensor(out, bet_t[t][:].indirect(lists), scaled[t % 2][:, lo:hi], ADD)
+            nc.vector.tensor_tensor(out, bet_t[t][:].indirect(lists), scaled[t][:, lo:hi], ADD)
 
         def shift_high(t, a):
             shift(z_high[a][:, (t - 2) * HALF : (t - 1) * HALF], t, a * HALF, (a + 1) * HALF)
@@ -163,24 +162,36 @@ def tile_picked_filmres_silu_po_kernel(
             cols = slice(u * UNIT, (u + 1) * UNIT)
             inner = (u % 2) * UNIT
             weave_pair(u, 1, z_high[u // 2][:].rearrange("p (t c) -> p t c", t=2)[:, :, inner : inner + UNIT])
-            quantise(z_w[:, cols], z_s[:, cols], z_woven[u])
+            quantise(z_w[:, cols], z_s[:, cols], z_woven[u][:])
             for t in range(PACK):
                 product(second_acc[u][:, t, :], w2, s2, t, z_w[:, cols], z_s[:, cols])
 
         scale(0)
         scale(1)
-        nc.vector.tensor_tensor(z_low[:, 0, :], shift0[:], scaled[0][:], ADD)
+        turned_acc = psum.tile([P, S], F32, name="turned_acc", tag="bank5")
+        back_acc = psum.tile([P, S], F32, name="back_acc", tag="bank6")
+        turned = tile("turned", [P, S], F32)
+        for u in range(units):
+            cols = slice(u * UNIT, (u + 1) * UNIT)
+            for k, term in enumerate((shift0, scaled[0])):
+                nc.tensor.matmul(turned_acc[:, cols], lhsT=term[:, cols], rhs=identity[:], is_transpose=True, start=k == 0, stop=k == 1)
+        nc.scalar.copy(out=turned[:], in_=turned_acc[:])
+        for u in range(units):
+            cols = slice(u * UNIT, (u + 1) * UNIT)
+            nc.tensor.transpose(back_acc[:, cols], turned[:, cols], identity[:])
+        nc.scalar.copy(out=z_low[:, 0, :], in_=back_acc[:])
+        scale(2)
         shift(z_low[:, 1, :], 1, 0, S)
         for u in range(units):
             weave_pair(u, 0, z_low[:, :, u * UNIT : (u + 1) * UNIT])
         deal(s2[:], s2_raw[:])
-        scale(2)
         scale(3)
         shift_high(2, 0)
         shift_high(3, 0)
         shift_high(2, 1)
         shift_high(3, 1)
-        multiply(0)
+        for u in range(units):
+            multiply(u)
 
         def add_residual(u):
             cols = slice(u * UNIT, (u + 1) * UNIT)
@@ -199,8 +210,6 @@ def tile_picked_filmres_silu_po_kernel(
             nc.sync.dma_start(out=words_of(out_1)[:, cols], in_=y_w[:, cols].bitcast(I32))
 
         for u in range(units):
-            if u + 1 < units:
-                multiply(u + 1)
             add_residual(u)
         hand_on(0, HALF)
         hand_on(HALF, S - UNIT)

@@ -16,12 +16,15 @@ SILU = mybir.ActivationFunctionType.Silu
 
 P = 128
 PACK = 4
-QUADS = 4
+QUAD = 32
+ROWS = 4
 TOKENS = 2048
 S = 512
 W = 512
 HALF = S // 2
 UNIT = 128
+UNITS = S // UNIT
+LAST = PACK - 1
 FLOPS = 2 * 2 * 512 * 512 * 512
 
 
@@ -37,16 +40,17 @@ def tile_picked_filmres_silu_po_kernel(
         return dram.rearrange("(p t) c -> p t c", t=PACK)
 
     def scale_rows(plane, dram, r):
-        return plane[r:P:32, :].bitcast(I32), dram[0, r : 4 * QUADS : 4, :].bitcast(I32)
+        return plane[r:P:QUAD, :].bitcast(I32), dram[0, r : ROWS * P // QUAD : ROWS, :].bitcast(I32)
 
-    def load_scales(plane, dram, queue=nc.sync):
-        for r in range(4):
+    def load_scales(plane, dram):
+        for r in range(ROWS):
             rows, source = scale_rows(plane, dram, r)
-            queue.dma_start(out=rows, in_=source)
+            nc.sync.dma_start(out=rows, in_=source)
 
     def deal(dst, src, lo=0, hi=PACK):
         nc.vector.tensor_copy(
-            out=dst.rearrange("p (t m) -> p m t", t=PACK)[:, :, lo:hi], in_=src.rearrange("p (m t) -> p m t", t=PACK)[:, :, lo:hi]
+            out=dst.rearrange("p (t m) -> p m t", t=PACK)[:, :, lo:hi],
+            in_=src.rearrange("p (m t) -> p m t", t=PACK)[:, :, lo:hi],
         )
 
     def weave(copy, dst, src):
@@ -74,6 +78,9 @@ def tile_picked_filmres_silu_po_kernel(
         def tile(name, shape, dtype):
             return keep.tile(shape, dtype, name=name, align_bytes=64)
 
+        def bank(name, shape, number):
+            return psum.tile(shape, F32, name=name, tag="bank%d" % number)
+
         offs_t = tile("offs_t", [P, S // 16], U16)
         task_t = tile("task_t", [P, S // 16], U16)
         x_w = tile("x_w", [P, TOKENS], U32)
@@ -84,14 +91,15 @@ def tile_picked_filmres_silu_po_kernel(
         s2_raw = tile("s2_raw", [P, W], U8)
         res_t = tile("res_t", [P, PACK, S], F32)
         gam_t = [tile("gam%d" % t, [P, 2 * W], F32) for t in range(PACK)]
-        bet_t = [tile("bet%d" % t, [P, W if t >= 2 else 2 * W], F32) for t in range(PACK)]
+        bet_t = [tile("bet%d" % t, [P, W if t == LAST else 2 * W], F32) for t in range(PACK)]
 
         nc.vector.memset(x_s[:].bitcast(I32), 0)
-        nc.gpsimd.memset(s1_raw[:].bitcast(I32), 0)
-        nc.gpsimd.memset(s2_raw[:].bitcast(I32), 0)
+        nc.vector.memset(s1_raw[:].bitcast(I32), 0)
+        nc.vector.memset(s2_raw[:].bitcast(I32), 0)
 
         identity = tile("identity", [P, P], F32)
-        make_identity(nc, identity[:])
+        nc.vector.memset(identity[:], 0.0)
+        make_identity(nc, identity[:], nomemset=True)
 
         def load_plane(tiles, dram, t):
             nc.sync.dma_start(out=tiles[t][:, 0:W], in_=planes_of(dram)[:, t, :])
@@ -129,16 +137,16 @@ def tile_picked_filmres_silu_po_kernel(
         nc.vector.tensor_copy(shift0[:], bet_t[0][:].indirect(task_t[:]))
         deal(w2[:], w2_raw[:])
         h = [tile("h%d" % t, [P, S], F32) for t in range(PACK)]
-        for bank, (t, lo, hi) in enumerate([(0, 0, HALF), (0, HALF, S), (1, 0, S), (2, 0, S), (3, 0, S)]):
-            first_acc = psum.tile([P, hi - lo], F32, name="first_acc%d" % bank, tag="bank%d" % bank)
+        passes = [(0, 0, HALF), (0, HALF, S)] + [(t, 0, S) for t in range(1, PACK)]
+        for number, (t, lo, hi) in enumerate(passes):
+            first_acc = bank("first_acc%d" % number, [P, hi - lo], number)
             product(first_acc[:], w1, s1, t, picked_w[:, lo:hi], picked_s[:, lo:hi])
             nc.scalar.activation(out=h[t][:, lo:hi], in_=first_acc[:], func=SILU)
 
-        units = S // UNIT
         z_low = tile("z_low", [P, 2, S], F32)
-        z_high = [tile("z_high%d" % a, [P, 2 * HALF], F32) for a in range(2)]
+        z_high = tile("z_high", [P, 2 * S], F32)
         scaled = [tile("scaled%d" % i, [P, S], F32) for i in range(PACK)]
-        z_woven = [tile("z_woven%d" % u, [P, UNIT, PACK], BF16) for u in range(units)]
+        z_woven = [tile("z_woven%d" % u, [P, UNIT, PACK], BF16) for u in range(UNITS)]
 
         def scale(t):
             nc.vector.tensor_tensor(scaled[t][:], gam_t[t][:].indirect(task_t[:]), h[t][:], MULT)
@@ -147,8 +155,8 @@ def tile_picked_filmres_silu_po_kernel(
             lists = task_t[:, lo // 16 : hi // 16]
             nc.vector.tensor_tensor(out, bet_t[t][:].indirect(lists), scaled[t][:, lo:hi], ADD)
 
-        def shift_high(t, a):
-            shift(z_high[a][:, (t - 2) * HALF : (t - 1) * HALF], t, a * HALF, (a + 1) * HALF)
+        def shift_high(t, lo, hi):
+            shift(z_high[:, (t - 2) * S + lo : (t - 2) * S + hi], t, lo, hi)
 
         def weave_pair(u, pair, src):
             nc.scalar.copy(out=z_woven[u][:, :, 2 * pair : 2 * pair + 2], in_=src.rearrange("p t c -> p c t"))
@@ -156,41 +164,42 @@ def tile_picked_filmres_silu_po_kernel(
         z_w, z_s = tile("z_w", [P, S], U32), tile("z_s", [P, S], U8)
         y_w, y_s = tile("y_w", [P, S], U32), tile("y_s", [P, S], U8)
         y_woven = tile("y_woven", [P, S, PACK], BF16)
-        second_acc = [psum.tile([P, PACK, UNIT], F32, name="second_acc%d" % u, tag="bank%d" % u) for u in range(units)]
+        second_acc = [bank("second_acc%d" % u, [P, PACK, UNIT], u) for u in range(UNITS)]
 
         def multiply(u):
             cols = slice(u * UNIT, (u + 1) * UNIT)
-            inner = (u % 2) * UNIT
-            weave_pair(u, 1, z_high[u // 2][:].rearrange("p (t c) -> p t c", t=2)[:, :, inner : inner + UNIT])
+            weave_pair(u, 1, z_high[:].rearrange("p (t c) -> p t c", t=2)[:, :, cols])
             quantise(z_w[:, cols], z_s[:, cols], z_woven[u][:])
             for t in range(PACK):
                 product(second_acc[u][:, t, :], w2, s2, t, z_w[:, cols], z_s[:, cols])
 
         scale(0)
         scale(1)
-        turned_acc = psum.tile([P, S], F32, name="turned_acc", tag="bank5")
-        back_acc = psum.tile([P, S], F32, name="back_acc", tag="bank6")
+        turned_acc = bank("turned_acc", [P, S], len(passes))
+        back_acc = bank("back_acc", [P, S], len(passes) + 1)
         turned = tile("turned", [P, S], F32)
-        for u in range(units):
+        for u in range(UNITS):
             cols = slice(u * UNIT, (u + 1) * UNIT)
             for k, term in enumerate((shift0, scaled[0])):
-                nc.tensor.matmul(turned_acc[:, cols], lhsT=term[:, cols], rhs=identity[:], is_transpose=True, start=k == 0, stop=k == 1)
+                nc.tensor.matmul(
+                    turned_acc[:, cols], lhsT=term[:, cols], rhs=identity[:], is_transpose=True, start=k == 0, stop=k == 1
+                )
         nc.scalar.copy(out=turned[:], in_=turned_acc[:])
-        for u in range(units):
+        for u in range(UNITS):
             cols = slice(u * UNIT, (u + 1) * UNIT)
             nc.tensor.transpose(back_acc[:, cols], turned[:, cols], identity[:])
         nc.scalar.copy(out=z_low[:, 0, :], in_=back_acc[:])
         scale(2)
         shift(z_low[:, 1, :], 1, 0, S)
-        for u in range(units):
+        for u in range(UNITS):
             weave_pair(u, 0, z_low[:, :, u * UNIT : (u + 1) * UNIT])
         deal(s2[:], s2_raw[:])
-        scale(3)
-        shift_high(2, 0)
-        shift_high(3, 0)
-        shift_high(2, 1)
-        shift_high(3, 1)
-        for u in range(units):
+        scale(LAST)
+        shift_high(2, 0, S)
+        shift_high(LAST, 0, HALF)
+        shift_high(LAST, HALF, S)
+
+        for u in range(UNITS):
             multiply(u)
 
         def add_residual(u):
@@ -198,7 +207,7 @@ def tile_picked_filmres_silu_po_kernel(
             y = tile("y%d" % u, [P, PACK, UNIT], F32)
             nc.vector.tensor_tensor(y[:], second_acc[u][:], res_t[:, :, cols], ADD)
             nc.sync.dma_start(out=planes_of(out_0)[:, :, cols], in_=y[:])
-            copies = [nc.scalar.copy, nc.vector.tensor_copy] if u == units - 1 else [nc.scalar.copy]
+            copies = [nc.scalar.copy, nc.vector.tensor_copy] if u == UNITS - 1 else [nc.scalar.copy]
             share = UNIT // len(copies)
             for e, copy in enumerate(copies):
                 lo = u * UNIT + e * share
@@ -209,11 +218,11 @@ def tile_picked_filmres_silu_po_kernel(
             quantise(y_w[:, cols], y_s[:, cols], y_woven[:, cols, :])
             nc.sync.dma_start(out=words_of(out_1)[:, cols], in_=y_w[:, cols].bitcast(I32))
 
-        for u in range(units):
+        for u in range(UNITS):
             add_residual(u)
         hand_on(0, HALF)
         hand_on(HALF, S - UNIT)
         hand_on(S - UNIT, S)
-        for q in range(QUADS):
-            rows, target = scale_rows(y_s, out_2, q)
-            (nc.sync if q == 0 else nc.scalar).dma_start(out=target, in_=rows)
+        for r in range(ROWS):
+            rows, target = scale_rows(y_s, out_2, r)
+            (nc.sync if r == 0 else nc.scalar).dma_start(out=target, in_=rows)

@@ -42,8 +42,8 @@ def tile_picked_filmres_silu_po_kernel(
     def scale_rows(plane, dram, r):
         return plane[r:P:QUAD, :].bitcast(I32), dram[0, r : ROWS * P // QUAD : ROWS, :].bitcast(I32)
 
-    def load_scales(plane, dram):
-        for r in range(ROWS):
+    def load_scales(plane, dram, lo=0, hi=ROWS):
+        for r in range(lo, hi):
             rows, source = scale_rows(plane, dram, r)
             nc.sync.dma_start(out=rows, in_=source)
 
@@ -91,7 +91,7 @@ def tile_picked_filmres_silu_po_kernel(
         s2_raw = tile("s2_raw", [P, W], U8)
         res_t = tile("res_t", [P, PACK, S], F32)
         gam_t = [tile("gam%d" % t, [P, 2 * W], F32) for t in range(PACK)]
-        bet_t = [tile("bet%d" % t, [P, W if t == LAST else 2 * W], F32) for t in range(PACK)]
+        bet_t = [tile("bet%d" % t, [P, W if t >= 2 else 2 * W], F32) for t in range(PACK)]
 
         nc.vector.memset(x_s[:].bitcast(I32), 0)
         nc.vector.memset(s1_raw[:].bitcast(I32), 0)
@@ -119,10 +119,13 @@ def tile_picked_filmres_silu_po_kernel(
         nc.sync.dma_start(out=w2_raw[:], in_=words_of(w2_words))
         load_plane(gam_t, gam, 0)
         load_plane(gam_t, gam, 1)
-        load_scales(s2_raw, w2_scales)
-        for tiles, dram, t in ((gam_t, gam, 2), (bet_t, bet, 1), (gam_t, gam, 3), (bet_t, bet, 2), (bet_t, bet, 3)):
+        load_scales(s2_raw, w2_scales, 0, ROWS - 1)
+        for tiles, dram, t in ((gam_t, gam, 2), (bet_t, bet, 1), (gam_t, gam, 3)):
             load_plane(tiles, dram, t)
         nc.sync.dma_start(out=res_t[:], in_=planes_of(res))
+        load_plane(bet_t, bet, 2)
+        load_plane(bet_t, bet, 3)
+        load_scales(s2_raw, w2_scales, ROWS - 1)
 
         picked_s = tile("picked_s", [P, S], U8)
         picked_w = tile("picked_w", [P, S], U32)
@@ -144,7 +147,7 @@ def tile_picked_filmres_silu_po_kernel(
             nc.scalar.activation(out=h[t][:, lo:hi], in_=first_acc[:], func=SILU)
 
         z_low = tile("z_low", [P, 2, S], F32)
-        z_high = tile("z_high", [P, 2 * S], F32)
+        z_high = tile("z_high", [P, 3, HALF], F32)
         scaled = [tile("scaled%d" % i, [P, S], F32) for i in range(PACK)]
         z_woven = [tile("z_woven%d" % u, [P, UNIT, PACK], BF16) for u in range(UNITS)]
 
@@ -155,8 +158,8 @@ def tile_picked_filmres_silu_po_kernel(
             lists = task_t[:, lo // 16 : hi // 16]
             nc.vector.tensor_tensor(out, bet_t[t][:].indirect(lists), scaled[t][:, lo:hi], ADD)
 
-        def shift_high(t, lo, hi):
-            shift(z_high[:, (t - 2) * S + lo : (t - 2) * S + hi], t, lo, hi)
+        def shift_high(t, half):
+            shift(z_high[:, (t - 2) * (1 + half), :], t, half * HALF, (half + 1) * HALF)
 
         def weave_pair(u, pair, src):
             nc.scalar.copy(out=z_woven[u][:, :, 2 * pair : 2 * pair + 2], in_=src.rearrange("p t c -> p c t"))
@@ -168,7 +171,8 @@ def tile_picked_filmres_silu_po_kernel(
 
         def multiply(u):
             cols = slice(u * UNIT, (u + 1) * UNIT)
-            weave_pair(u, 1, z_high[:].rearrange("p (t c) -> p t c", t=2)[:, :, cols])
+            half, lo = divmod(u * UNIT, HALF)
+            weave_pair(u, 1, z_high[:, 0 : 2 + half : 1 + half, lo : lo + UNIT])
             quantise(z_w[:, cols], z_s[:, cols], z_woven[u][:])
             for t in range(PACK):
                 product(second_acc[u][:, t, :], w2, s2, t, z_w[:, cols], z_s[:, cols])
@@ -193,14 +197,14 @@ def tile_picked_filmres_silu_po_kernel(
         shift(z_low[:, 1, :], 1, 0, S)
         for u in range(UNITS):
             weave_pair(u, 0, z_low[:, :, u * UNIT : (u + 1) * UNIT])
-        deal(s2[:], s2_raw[:])
         scale(LAST)
-        shift_high(2, 0, S)
-        shift_high(LAST, 0, HALF)
-        shift_high(LAST, HALF, S)
-
-        for u in range(UNITS):
-            multiply(u)
+        shift_high(2, 0)
+        shift_high(LAST, 0)
+        shift_high(LAST, 1)
+        deal(s2[:], s2_raw[:])
+        multiply(0)
+        multiply(1)
+        shift_high(2, 1)
 
         def add_residual(u):
             cols = slice(u * UNIT, (u + 1) * UNIT)
@@ -218,7 +222,10 @@ def tile_picked_filmres_silu_po_kernel(
             quantise(y_w[:, cols], y_s[:, cols], y_woven[:, cols, :])
             nc.sync.dma_start(out=words_of(out_1)[:, cols], in_=y_w[:, cols].bitcast(I32))
 
-        for u in range(UNITS):
+        add_residual(0)
+        multiply(2)
+        multiply(3)
+        for u in range(1, UNITS):
             add_residual(u)
         hand_on(0, HALF)
         hand_on(HALF, S - UNIT)

@@ -116,16 +116,15 @@ def tile_picked_filmres_silu_po_kernel(
         load_scales(s1_raw, w1_scales)
         nc.sync.dma_start(task_t[:], task)
         load_plane(bet_t, bet, 0)
-        nc.sync.dma_start(out=w2_raw[:], in_=words_of(w2_words))
-        load_plane(gam_t, gam, 0)
-        load_plane(gam_t, gam, 1)
-        load_scales(s2_raw, w2_scales, 0, ROWS - 1)
-        for tiles, dram, t in ((gam_t, gam, 2), (bet_t, bet, 1), (gam_t, gam, 3)):
+        for tiles, dram, t in ((gam_t, gam, 0), (gam_t, gam, 1), (gam_t, gam, 2), (bet_t, bet, 1), (gam_t, gam, 3)):
             load_plane(tiles, dram, t)
-        nc.sync.dma_start(out=res_t[:], in_=planes_of(res))
+        load_scales(s2_raw, w2_scales, 0, ROWS - 1)
         load_plane(bet_t, bet, 2)
         load_plane(bet_t, bet, 3)
         load_scales(s2_raw, w2_scales, ROWS - 1)
+        nc.sync.dma_start(out=w2_raw[:], in_=words_of(w2_words))
+        for lo, hi in ((0, UNIT), (UNIT, S)):
+            nc.sync.dma_start(out=res_t[:, :, lo:hi], in_=planes_of(res)[:, :, lo:hi])
 
         picked_s = tile("picked_s", [P, S], U8)
         picked_w = tile("picked_w", [P, S], U32)
@@ -138,7 +137,6 @@ def tile_picked_filmres_silu_po_kernel(
         deal(s1[:], s1_raw[:], 0, 1)
         deal(s1[:], s1_raw[:], 1, PACK)
         nc.vector.tensor_copy(shift0[:], bet_t[0][:].indirect(task_t[:]))
-        deal(w2[:], w2_raw[:])
         h = [tile("h%d" % t, [P, S], F32) for t in range(PACK)]
         passes = [(0, 0, HALF), (0, HALF, S)] + [(t, 0, S) for t in range(1, PACK)]
         for number, (t, lo, hi) in enumerate(passes):
@@ -169,10 +167,12 @@ def tile_picked_filmres_silu_po_kernel(
         y_woven = tile("y_woven", [P, S, PACK], BF16)
         second_acc = [bank("second_acc%d" % u, [P, PACK, UNIT], u) for u in range(UNITS)]
 
-        def multiply(u):
-            cols = slice(u * UNIT, (u + 1) * UNIT)
+        def round_high(u):
             half, lo = divmod(u * UNIT, HALF)
             weave_pair(u, 1, z_high[:, 0 : 2 + half : 1 + half, lo : lo + UNIT])
+
+        def multiply(u):
+            cols = slice(u * UNIT, (u + 1) * UNIT)
             quantise(z_w[:, cols], z_s[:, cols], z_woven[u][:])
             for t in range(PACK):
                 product(second_acc[u][:, t, :], w2, s2, t, z_w[:, cols], z_s[:, cols])
@@ -202,9 +202,14 @@ def tile_picked_filmres_silu_po_kernel(
         shift_high(LAST, 0)
         shift_high(LAST, 1)
         deal(s2[:], s2_raw[:])
+        deal(w2[:], w2_raw[:])
+        round_high(0)
+        round_high(1)
         multiply(0)
-        multiply(1)
         shift_high(2, 1)
+        round_high(2)
+        round_high(3)
+        multiply(1)
 
         def add_residual(u):
             cols = slice(u * UNIT, (u + 1) * UNIT)
@@ -220,7 +225,9 @@ def tile_picked_filmres_silu_po_kernel(
         def hand_on(lo, hi):
             cols = slice(lo, hi)
             quantise(y_w[:, cols], y_s[:, cols], y_woven[:, cols, :])
-            nc.sync.dma_start(out=words_of(out_1)[:, cols], in_=y_w[:, cols].bitcast(I32))
+
+        def store_words(lo, hi):
+            nc.sync.dma_start(out=words_of(out_1)[:, lo:hi], in_=y_w[:, lo:hi].bitcast(I32))
 
         add_residual(0)
         multiply(2)
@@ -229,7 +236,9 @@ def tile_picked_filmres_silu_po_kernel(
             add_residual(u)
         hand_on(0, HALF)
         hand_on(HALF, S - UNIT)
+        store_words(0, S - UNIT)
         hand_on(S - UNIT, S)
+        store_words(S - UNIT, S)
         for r in range(ROWS):
             rows, target = scale_rows(y_s, out_2, r)
             (nc.sync if r == 0 else nc.scalar).dma_start(out=target, in_=rows)

@@ -24,6 +24,7 @@ W = 512
 HALF = S // 2
 UNIT = 128
 UNITS = S // UNIT
+LAST_SHARE = 32
 LAST = PACK - 1
 FLOPS = 2 * 2 * 512 * 512 * 512
 
@@ -149,8 +150,9 @@ def tile_picked_filmres_silu_po_kernel(
         scaled = [tile("scaled%d" % i, [P, S], F32) for i in range(PACK)]
         z_woven = [tile("z_woven%d" % u, [P, UNIT, PACK], BF16) for u in range(UNITS)]
 
-        def scale(t):
-            nc.vector.tensor_tensor(scaled[t][:], gam_t[t][:].indirect(task_t[:]), h[t][:], MULT)
+        def scale(t, lo=0, hi=S):
+            lists = task_t[:, lo // 16 : hi // 16]
+            nc.vector.tensor_tensor(scaled[t][:, lo:hi], gam_t[t][:].indirect(lists), h[t][:, lo:hi], MULT)
 
         def shift(out, t, lo, hi):
             lists = task_t[:, lo // 16 : hi // 16]
@@ -159,17 +161,17 @@ def tile_picked_filmres_silu_po_kernel(
         def shift_high(t, half):
             shift(z_high[:, (t - 2) * (1 + half), :], t, half * HALF, (half + 1) * HALF)
 
-        def weave_pair(u, pair, src):
-            nc.scalar.copy(out=z_woven[u][:, :, 2 * pair : 2 * pair + 2], in_=src.rearrange("p t c -> p c t"))
+        def weave_pair(u, pair, src, copy=nc.scalar.copy):
+            copy(out=z_woven[u][:, :, 2 * pair : 2 * pair + 2], in_=src.rearrange("p t c -> p c t"))
 
         z_w, z_s = tile("z_w", [P, S], U32), tile("z_s", [P, S], U8)
         y_w, y_s = tile("y_w", [P, S], U32), tile("y_s", [P, S], U8)
         y_woven = tile("y_woven", [P, S, PACK], BF16)
         second_acc = [bank("second_acc%d" % u, [P, PACK, UNIT], u) for u in range(UNITS)]
 
-        def round_high(u):
+        def round_high(u, copy=nc.scalar.copy):
             half, lo = divmod(u * UNIT, HALF)
-            weave_pair(u, 1, z_high[:, 0 : 2 + half : 1 + half, lo : lo + UNIT])
+            weave_pair(u, 1, z_high[:, 0 : 2 + half : 1 + half, lo : lo + UNIT], copy)
 
         def multiply(u):
             cols = slice(u * UNIT, (u + 1) * UNIT)
@@ -177,7 +179,8 @@ def tile_picked_filmres_silu_po_kernel(
             for t in range(PACK):
                 product(second_acc[u][:, t, :], w2, s2, t, z_w[:, cols], z_s[:, cols])
 
-        scale(0)
+        scale(0, 0, HALF)
+        scale(0, HALF, S)
         scale(1)
         turned_acc = bank("turned_acc", [P, S], len(passes))
         back_acc = bank("back_acc", [P, S], len(passes) + 1)
@@ -192,35 +195,39 @@ def tile_picked_filmres_silu_po_kernel(
         for u in range(UNITS):
             cols = slice(u * UNIT, (u + 1) * UNIT)
             nc.tensor.transpose(back_acc[:, cols], turned[:, cols], identity[:])
-        nc.scalar.copy(out=z_low[:, 0, :], in_=back_acc[:])
+        nc.scalar.copy(out=z_low[:, 0, 0 : S - UNIT], in_=back_acc[:, 0 : S - UNIT])
         scale(2)
         shift(z_low[:, 1, :], 1, 0, S)
-        for u in range(UNITS):
+        for u in range(UNITS - 1):
             weave_pair(u, 0, z_low[:, :, u * UNIT : (u + 1) * UNIT])
+        nc.scalar.copy(out=z_woven[UNITS - 1][:, :, 1], in_=z_low[:, 1, S - UNIT : S])
+        nc.scalar.copy(out=z_woven[UNITS - 1][:, :, 0], in_=back_acc[:, S - UNIT : S])
         scale(LAST)
         shift_high(2, 0)
         shift_high(LAST, 0)
         shift_high(LAST, 1)
+        warm_acc = bank("warm_acc", [P, S], len(passes) + 1)
+        for t in range(2):
+            product(warm_acc[:], w1, s1, t, picked_w[:], picked_s[:])
         deal(s2[:], s2_raw[:])
         deal(w2[:], w2_raw[:])
         round_high(0)
         round_high(1)
         multiply(0)
         shift_high(2, 1)
-        round_high(2)
         round_high(3)
         multiply(1)
+        round_high(2, nc.vector.tensor_copy)
 
         def add_residual(u):
             cols = slice(u * UNIT, (u + 1) * UNIT)
             y = tile("y%d" % u, [P, PACK, UNIT], F32)
             nc.vector.tensor_tensor(y[:], second_acc[u][:], res_t[:, :, cols], ADD)
             nc.sync.dma_start(out=planes_of(out_0)[:, :, cols], in_=y[:])
-            copies = [nc.scalar.copy, nc.vector.tensor_copy] if u == UNITS - 1 else [nc.scalar.copy]
-            share = UNIT // len(copies)
-            for e, copy in enumerate(copies):
-                lo = u * UNIT + e * share
-                weave(copy, y_woven[:, lo : lo + share, :], y[:, :, e * share : (e + 1) * share])
+            share = LAST_SHARE if u == UNITS - 1 else UNIT
+            weave(nc.scalar.copy, y_woven[:, u * UNIT : u * UNIT + share, :], y[:, :, 0:share])
+            if share < UNIT:
+                weave(nc.vector.tensor_copy, y_woven[:, u * UNIT + share : S, :], y[:, :, share:UNIT])
 
         def hand_on(lo, hi):
             cols = slice(lo, hi)

@@ -121,8 +121,8 @@ def tile_picked_filmres_silu_po_kernel(
             load_plane(tiles, dram, t)
         load_scales(s2_raw, w2_scales, 0, ROWS - 1)
         load_plane(bet_t, bet, 2)
-        load_plane(bet_t, bet, 3)
         load_scales(s2_raw, w2_scales, ROWS - 1)
+        load_plane(bet_t, bet, 3)
         nc.sync.dma_start(out=w2_raw[:], in_=words_of(w2_words))
         for lo, hi in ((0, UNIT), (UNIT, S)):
             nc.sync.dma_start(out=res_t[:, :, lo:hi], in_=planes_of(res)[:, :, lo:hi])
@@ -146,7 +146,7 @@ def tile_picked_filmres_silu_po_kernel(
             nc.scalar.activation(out=h[t][:, lo:hi], in_=first_acc[:], func=SILU)
 
         z_low = tile("z_low", [P, 2, S], F32)
-        z_high = tile("z_high", [P, 3, HALF], F32)
+        z_high = tile("z_high", [P, 7, UNIT], F32)
         scaled = [tile("scaled%d" % i, [P, S], F32) for i in range(PACK)]
         z_woven = [tile("z_woven%d" % u, [P, UNIT, PACK], BF16) for u in range(UNITS)]
 
@@ -159,7 +159,8 @@ def tile_picked_filmres_silu_po_kernel(
             nc.vector.tensor_tensor(out, bet_t[t][:].indirect(lists), scaled[t][:, lo:hi], ADD)
 
         def shift_high(t, half):
-            shift(z_high[:, (t - 2) * (1 + half), :], t, half * HALF, (half + 1) * HALF)
+            row = 1 - half if t == 2 else 3 + 2 * half
+            shift(z_high[:, row : row + 2, :].rearrange("p u c -> p (u c)"), t, half * HALF, (half + 1) * HALF)
 
         def weave_pair(u, pair, src, copy=nc.scalar.copy):
             copy(out=z_woven[u][:, :, 2 * pair : 2 * pair + 2], in_=src.rearrange("p t c -> p c t"))
@@ -170,8 +171,8 @@ def tile_picked_filmres_silu_po_kernel(
         second_acc = [bank("second_acc%d" % u, [P, PACK, UNIT], u) for u in range(UNITS)]
 
         def round_high(u, copy=nc.scalar.copy):
-            half, lo = divmod(u * UNIT, HALF)
-            weave_pair(u, 1, z_high[:, 0 : 2 + half : 1 + half, lo : lo + UNIT], copy)
+            row = u + 1 if u < 2 else u - 2
+            weave_pair(u, 1, z_high[:, row : u + 4 : u + 3 - row, :], copy)
 
         def multiply(u):
             cols = slice(u * UNIT, (u + 1) * UNIT)
@@ -195,21 +196,19 @@ def tile_picked_filmres_silu_po_kernel(
         for u in range(UNITS):
             cols = slice(u * UNIT, (u + 1) * UNIT)
             nc.tensor.transpose(back_acc[:, cols], turned[:, cols], identity[:])
-        nc.scalar.copy(out=z_low[:, 0, 0 : S - UNIT], in_=back_acc[:, 0 : S - UNIT])
+        nc.scalar.copy(out=z_low[:, 0, :], in_=back_acc[:])
         scale(2)
         shift(z_low[:, 1, :], 1, 0, S)
-        for u in range(UNITS - 1):
+        for u in range(UNITS):
             weave_pair(u, 0, z_low[:, :, u * UNIT : (u + 1) * UNIT])
-        nc.scalar.copy(out=z_woven[UNITS - 1][:, :, 1], in_=z_low[:, 1, S - UNIT : S])
-        nc.scalar.copy(out=z_woven[UNITS - 1][:, :, 0], in_=back_acc[:, S - UNIT : S])
         scale(LAST)
         shift_high(2, 0)
         shift_high(LAST, 0)
+        deal(s2[:], s2_raw[:])
         shift_high(LAST, 1)
         warm_acc = bank("warm_acc", [P, S], len(passes) + 1)
         for t in range(2):
-            product(warm_acc[:], w1, s1, t, picked_w[:], picked_s[:])
-        deal(s2[:], s2_raw[:])
+            product(warm_acc[:], w1, s2, t, picked_w[:], picked_s[:])
         deal(w2[:], w2_raw[:])
         round_high(0)
         round_high(1)

@@ -48,6 +48,12 @@ def tile_picked_filmres_silu_po_kernel(
             rows, source = scale_rows(plane, dram, r)
             nc.sync.dma_start(out=rows, in_=source)
 
+    def deal_words(dst, src):
+        nc.scalar.copy(
+            out=dst.bitcast(U32).rearrange("p (t m) -> p m t", t=PACK),
+            in_=src.bitcast(U32).rearrange("p (m t) -> p m t", t=PACK),
+        )
+
     def deal(dst, src, lo=0, hi=PACK):
         nc.vector.tensor_copy(
             out=dst.rearrange("p (t m) -> p m t", t=PACK)[:, :, lo:hi],
@@ -100,6 +106,8 @@ def tile_picked_filmres_silu_po_kernel(
 
         identity = tile("identity", [P, P], F32)
         nc.vector.memset(identity[:], 0.0)
+        first = tile("first", [P, 1], F32)
+        nc.scalar.activation(out=first[:], in_=identity[:, 0:1], func=SILU)
         make_identity(nc, identity[:], nomemset=True)
 
         def load_plane(tiles, dram, t):
@@ -117,13 +125,15 @@ def tile_picked_filmres_silu_po_kernel(
         load_scales(s1_raw, w1_scales)
         nc.sync.dma_start(task_t[:], task)
         load_plane(bet_t, bet, 0)
-        for tiles, dram, t in ((gam_t, gam, 0), (gam_t, gam, 1), (gam_t, gam, 2), (bet_t, bet, 1), (gam_t, gam, 3)):
+        for tiles, dram, t in ((gam_t, gam, 0), (gam_t, gam, 1), (gam_t, gam, 2)):
             load_plane(tiles, dram, t)
+        nc.sync.dma_start(out=w2_raw[:], in_=words_of(w2_words))
+        load_plane(bet_t, bet, 1)
+        load_plane(gam_t, gam, 3)
         load_scales(s2_raw, w2_scales, 0, ROWS - 1)
         load_plane(bet_t, bet, 2)
-        load_scales(s2_raw, w2_scales, ROWS - 1)
         load_plane(bet_t, bet, 3)
-        nc.sync.dma_start(out=w2_raw[:], in_=words_of(w2_words))
+        load_scales(s2_raw, w2_scales, ROWS - 1)
         for lo, hi in ((0, UNIT), (UNIT, S)):
             nc.sync.dma_start(out=res_t[:, :, lo:hi], in_=planes_of(res)[:, :, lo:hi])
 
@@ -134,18 +144,19 @@ def tile_picked_filmres_silu_po_kernel(
         w2, s2 = tile("w2", [P, W], I32), tile("s2", [P, W], U8)
         nc.vector.tensor_copy(picked_s[:], x_s[:].indirect(offs_t[:]))
         nc.vector.tensor_copy(picked_w[:], x_w[:].indirect(offs_t[:]))
-        deal(w1[:], w1_raw[:])
+        deal_words(w1[:], w1_raw[:])
         deal(s1[:], s1_raw[:], 0, 1)
         deal(s1[:], s1_raw[:], 1, PACK)
         nc.vector.tensor_copy(shift0[:], bet_t[0][:].indirect(task_t[:]))
-        h = [tile("h%d" % t, [P, S], F32) for t in range(PACK)]
+        low = tile("low", [P, 2 * (2 * S - UNIT)], F32)
+        h = [tile("h%d" % t, [P, S], F32) for t in range(LAST)] + [low[:, S - UNIT : 2 * S - UNIT]]
         passes = [(0, 0, HALF), (0, HALF, S)] + [(t, 0, S) for t in range(1, PACK)]
         for number, (t, lo, hi) in enumerate(passes):
             first_acc = bank("first_acc%d" % number, [P, hi - lo], number)
             product(first_acc[:], w1, s1, t, picked_w[:, lo:hi], picked_s[:, lo:hi])
             nc.scalar.activation(out=h[t][:, lo:hi], in_=first_acc[:], func=SILU)
 
-        z_low = tile("z_low", [P, 2, S], F32)
+        z_low = low[:].rearrange("p (t c) -> p t c", t=2)
         z_high = tile("z_high", [P, 7, UNIT], F32)
         scaled = [tile("scaled%d" % i, [P, S], F32) for i in range(PACK)]
         z_woven = [tile("z_woven%d" % u, [P, UNIT, PACK], BF16) for u in range(UNITS)]
@@ -196,20 +207,22 @@ def tile_picked_filmres_silu_po_kernel(
         for u in range(UNITS):
             cols = slice(u * UNIT, (u + 1) * UNIT)
             nc.tensor.transpose(back_acc[:, cols], turned[:, cols], identity[:])
-        nc.scalar.copy(out=z_low[:, 0, :], in_=back_acc[:])
+        nc.scalar.copy(out=z_low[:, 0, 0 : S - UNIT], in_=back_acc[:, 0 : S - UNIT])
+        deal_words(w2[:], w2_raw[:])
         scale(2)
-        shift(z_low[:, 1, :], 1, 0, S)
-        for u in range(UNITS):
-            weave_pair(u, 0, z_low[:, :, u * UNIT : (u + 1) * UNIT])
+        shift(z_low[:, 1, 0:S], 1, 0, S)
         scale(LAST)
+        for u in range(UNITS):
+            if u == UNITS - 1:
+                nc.scalar.copy(out=z_low[:, 0, S - UNIT : S], in_=back_acc[:, S - UNIT : S])
+            weave_pair(u, 0, z_low[:, :, u * UNIT : (u + 1) * UNIT])
         shift_high(2, 0)
         shift_high(LAST, 0)
-        deal(s2[:], s2_raw[:])
         shift_high(LAST, 1)
+        deal(s2[:], s2_raw[:])
         warm_acc = bank("warm_acc", [P, S], len(passes) + 1)
         for t in range(2):
-            product(warm_acc[:], w1, s2, t, picked_w[:], picked_s[:])
-        deal(w2[:], w2_raw[:])
+            product(warm_acc[:], w1, s1, t, picked_w[:], picked_s[:])
         round_high(0)
         round_high(1)
         multiply(0)

@@ -139,9 +139,9 @@ def tile_picked_filmres_silu_po_kernel(
 
         picked_s = tile("picked_s", [P, S], U8)
         picked_w = tile("picked_w", [P, S], U32)
-        shift0 = tile("shift0", [P, S], F32)
+        shift0 = keep.tile([P, S], F32, name="shift0", tag="shift0", align_bytes=64)
         w1, s1 = tile("w1", [P, W], I32), tile("s1", [P, W], U8)
-        w2, s2 = tile("w2", [P, W], I32), tile("s2", [P, W], U8)
+        s2 = tile("s2", [P, W], U8)
         nc.vector.tensor_copy(picked_s[:], x_s[:].indirect(offs_t[:]))
         nc.vector.tensor_copy(picked_w[:], x_w[:].indirect(offs_t[:]))
         deal_words(w1[:], w1_raw[:])
@@ -158,8 +158,8 @@ def tile_picked_filmres_silu_po_kernel(
 
         z_low = low[:].rearrange("p (t c) -> p t c", t=2)
         z_high = tile("z_high", [P, 7, UNIT], F32)
-        scaled = [tile("scaled%d" % i, [P, S], F32) for i in range(PACK)]
-        z_woven = [tile("z_woven%d" % u, [P, UNIT, PACK], BF16) for u in range(UNITS)]
+        scaled = [keep.tile([P, S], F32, name="scaled%d" % i, tag="scaled%d" % i, align_bytes=64) for i in range(PACK)]
+        z_woven = [tile("z_woven%d" % u, [P, UNIT, PACK], BF16) for u in range(UNITS - 1)]
 
         def scale(t, lo=0, hi=S):
             lists = task_t[:, lo // 16 : hi // 16]
@@ -204,16 +204,17 @@ def tile_picked_filmres_silu_po_kernel(
                     turned_acc[:, cols], lhsT=term[:, cols], rhs=identity[:], is_transpose=True, start=k == 0, stop=k == 1
                 )
         nc.scalar.copy(out=turned[:], in_=turned_acc[:])
+        w2 = keep.tile([P, W], I32, name="w2", tag="shift0", align_bytes=64)
+        deal_words(w2[:], w2_raw[:])
         for u in range(UNITS):
             cols = slice(u * UNIT, (u + 1) * UNIT)
             nc.tensor.transpose(back_acc[:, cols], turned[:, cols], identity[:])
         nc.scalar.copy(out=z_low[:, 0, 0 : S - UNIT], in_=back_acc[:, 0 : S - UNIT])
-        deal_words(w2[:], w2_raw[:])
         scale(2)
         shift(z_low[:, 1, 0:S], 1, 0, S)
         scale(LAST)
-        for u in range(UNITS):
-            if u == UNITS - 1:
+        for u in range(UNITS - 1):
+            if u == 2:
                 nc.scalar.copy(out=z_low[:, 0, S - UNIT : S], in_=back_acc[:, S - UNIT : S])
             weave_pair(u, 0, z_low[:, :, u * UNIT : (u + 1) * UNIT])
         shift_high(2, 0)
@@ -225,6 +226,8 @@ def tile_picked_filmres_silu_po_kernel(
             product(warm_acc[:], w1, s1, t, picked_w[:], picked_s[:])
         round_high(0)
         round_high(1)
+        z_woven.append(keep.tile([P, UNIT, PACK], BF16, name="z_woven3", tag="scaled3", align_bytes=64))
+        weave_pair(UNITS - 1, 0, z_low[:, :, S - UNIT : S])
         multiply(0)
         shift_high(2, 1)
         round_high(3)

@@ -1,7 +1,6 @@
 from contextlib import ExitStack
 
 import concourse.mybir as mybir
-from concourse.masks import make_identity
 
 F32 = mybir.dt.float32
 BF16 = mybir.dt.bfloat16
@@ -13,6 +12,7 @@ FP8X4 = mybir.dt.float8_e4m3fn_x4
 MULT = mybir.AluOpType.mult
 ADD = mybir.AluOpType.add
 SILU = mybir.ActivationFunctionType.Silu
+COPY = mybir.ActivationFunctionType.Copy
 
 P = 128
 PACK = 4
@@ -25,7 +25,6 @@ HALF = S // 2
 UNIT = 128
 UNITS = S // UNIT
 LAST_SHARE = 32
-LAST = PACK - 1
 FLOPS = 2 * 2 * 512 * 512 * 512
 
 
@@ -48,20 +47,17 @@ def tile_picked_filmres_silu_po_kernel(
             rows, source = scale_rows(plane, dram, r)
             nc.sync.dma_start(out=rows, in_=source)
 
-    def deal_words(dst, src):
-        nc.scalar.copy(
-            out=dst.bitcast(U32).rearrange("p (t m) -> p m t", t=PACK),
-            in_=src.bitcast(U32).rearrange("p (m t) -> p m t", t=PACK),
-        )
-
-    def deal(dst, src, lo=0, hi=PACK):
-        nc.vector.tensor_copy(
+    def deal(copy, dst, src, lo=0, hi=PACK):
+        copy(
             out=dst.rearrange("p (t m) -> p m t", t=PACK)[:, :, lo:hi],
             in_=src.rearrange("p (m t) -> p m t", t=PACK)[:, :, lo:hi],
         )
 
-    def weave(copy, dst, src):
-        copy(out=dst.rearrange("p (c i) t -> p c t i", i=4), in_=src.rearrange("p t (c i) -> p c t i", i=4))
+    def woven(ap):
+        return ap.rearrange("p (c i) t -> p c t i", i=4)
+
+    def by_planes(ap):
+        return ap.rearrange("p t (c i) -> p c t i", i=4)
 
     def product(acc, weights, weight_scales, t, codes, scales):
         rows = slice(t * P, (t + 1) * P)
@@ -75,8 +71,8 @@ def tile_picked_filmres_silu_po_kernel(
             stop=True,
         )
 
-    def quantise(codes, scales, woven):
-        nc.vector.quantize_mx(out=codes.bitcast(FP8X4), scales=scales, in_=woven.rearrange("p c t -> p (c t)"))
+    def quantise(codes, scales, rounded):
+        nc.vector.quantize_mx(out=codes.bitcast(FP8X4), scales=scales, in_=rounded.rearrange("p c t -> p (c t)"))
 
     with ExitStack() as ctx:
         keep = ctx.enter_context(tc.tile_pool(name="keep", bufs=1))
@@ -92,23 +88,21 @@ def tile_picked_filmres_silu_po_kernel(
         task_t = tile("task_t", [P, S // 16], U16)
         x_w = tile("x_w", [P, TOKENS], U32)
         x_s = tile("x_s", [P, TOKENS], U8)
-        w1_raw = tile("w1_raw", [P, W], I32)
-        w2_raw = tile("w2_raw", [P, W], I32)
+        w1_raw = tile("w1_raw", [P, W], U32)
+        w2_raw = tile("w2_raw", [P, W], U32)
         s1_raw = tile("s1_raw", [P, W], U8)
         s2_raw = tile("s2_raw", [P, W], U8)
-        res_t = tile("res_t", [P, PACK, S], F32)
+        res_t = [tile("res%d" % a, [P, PACK, HALF], F32) for a in range(2)]
         gam_t = [tile("gam%d" % t, [P, 2 * W], F32) for t in range(PACK)]
-        bet_t = [tile("bet%d" % t, [P, W if t >= 2 else 2 * W], F32) for t in range(PACK)]
+        bet_t = [tile("bet%d" % t, [P, W if t == PACK - 1 else 2 * W], F32) for t in range(PACK)]
 
         nc.vector.memset(x_s[:].bitcast(I32), 0)
         nc.vector.memset(s1_raw[:].bitcast(I32), 0)
         nc.vector.memset(s2_raw[:].bitcast(I32), 0)
-
-        identity = tile("identity", [P, P], F32)
-        nc.vector.memset(identity[:], 0.0)
+        zero = tile("zero", [P, 1], F32)
         first = tile("first", [P, 1], F32)
-        nc.scalar.activation(out=first[:], in_=identity[:, 0:1], func=SILU)
-        make_identity(nc, identity[:], nomemset=True)
+        nc.vector.memset(zero[:], 0.0)
+        nc.scalar.activation(out=first[:], in_=zero[:], func=SILU)
 
         def load_plane(tiles, dram, t):
             nc.sync.dma_start(out=tiles[t][:, 0:W], in_=planes_of(dram)[:, t, :])
@@ -118,72 +112,70 @@ def tile_picked_filmres_silu_po_kernel(
             nc.sync.dma_start(out=x_w[:].bitcast(I32)[:, cols], in_=words_of(x_words)[:, cols])
 
         nc.sync.dma_start(offs_t[:], offs)
+        nc.sync.dma_start(task_t[:], task)
         load_x_half(0)
         load_scales(x_s, x_scales)
         load_x_half(1)
-        nc.sync.dma_start(out=w1_raw[:], in_=words_of(w1_words))
+        nc.sync.dma_start(out=w1_raw[:].bitcast(I32), in_=words_of(w1_words))
         load_scales(s1_raw, w1_scales)
-        nc.sync.dma_start(task_t[:], task)
-        load_plane(bet_t, bet, 0)
-        for tiles, dram, t in ((gam_t, gam, 0), (gam_t, gam, 1), (gam_t, gam, 2)):
+        for tiles, dram, t in ((bet_t, bet, 0), (gam_t, gam, 0), (gam_t, gam, 1)):
             load_plane(tiles, dram, t)
-        nc.sync.dma_start(out=w2_raw[:], in_=words_of(w2_words))
-        load_plane(bet_t, bet, 1)
-        load_plane(gam_t, gam, 3)
-        load_scales(s2_raw, w2_scales, 0, ROWS - 1)
-        load_plane(bet_t, bet, 2)
+        for r, (tiles, dram, t) in enumerate(((gam_t, gam, 2), (gam_t, gam, 3), (bet_t, bet, 1), (bet_t, bet, 2))):
+            load_plane(tiles, dram, t)
+            load_scales(s2_raw, w2_scales, r, r + 1)
         load_plane(bet_t, bet, 3)
-        load_scales(s2_raw, w2_scales, ROWS - 1)
-        for lo, hi in ((0, UNIT), (UNIT, S)):
-            nc.sync.dma_start(out=res_t[:, :, lo:hi], in_=planes_of(res)[:, :, lo:hi])
+        nc.sync.dma_start(out=w2_raw[:].bitcast(I32), in_=words_of(w2_words))
+        for a in range(2):
+            nc.sync.dma_start(out=res_t[a][:], in_=planes_of(res)[:, :, a * HALF : (a + 1) * HALF])
 
         picked_s = tile("picked_s", [P, S], U8)
         picked_w = tile("picked_w", [P, S], U32)
-        shift0 = keep.tile([P, S], F32, name="shift0", tag="shift0", align_bytes=64)
-        w1, s1 = tile("w1", [P, W], I32), tile("s1", [P, W], U8)
-        s2 = tile("s2", [P, W], U8)
+        w1, s1 = tile("w1", [P, W], U32), tile("s1", [P, W], U8)
+        w2, s2 = tile("w2", [P, W], U32), tile("s2", [P, W], U8)
         nc.vector.tensor_copy(picked_s[:], x_s[:].indirect(offs_t[:]))
         nc.vector.tensor_copy(picked_w[:], x_w[:].indirect(offs_t[:]))
-        deal_words(w1[:], w1_raw[:])
-        deal(s1[:], s1_raw[:], 0, 1)
-        deal(s1[:], s1_raw[:], 1, PACK)
-        nc.vector.tensor_copy(shift0[:], bet_t[0][:].indirect(task_t[:]))
-        low = tile("low", [P, 2 * (2 * S - UNIT)], F32)
-        h = [tile("h%d" % t, [P, S], F32) for t in range(LAST)] + [low[:, S - UNIT : 2 * S - UNIT]]
+        deal(nc.vector.tensor_copy, s1[:], s1_raw[:], 0, 1)
+        deal(nc.vector.tensor_copy, s1[:], s1_raw[:], 1, PACK)
+        deal(nc.scalar.copy, w1[:], w1_raw[:], 0, 1)
+        deal(nc.scalar.copy, w1[:], w1_raw[:], 1, PACK)
+        scaled = tile("scaled", [P, PACK * S], F32)[:].rearrange("p (t c) -> p t c", t=PACK)
+        shift = tile("shift", [P, PACK * S], F32)[:].rearrange("p (t c) -> p t c", t=PACK)
+
+        def look_up_shift(t, lo, hi):
+            nc.scalar.activation(shift[:, t, lo:hi], bet_t[t][:].indirect(task_t[:, lo // 16 : hi // 16]), COPY)
+
+        nc.vector.tensor_copy(shift[:, 0, :], bet_t[0][:].indirect(task_t[:]))
+
+        h = [tile("h%d" % t, [P, S], F32) for t in range(PACK)]
         passes = [(0, 0, HALF), (0, HALF, S)] + [(t, 0, S) for t in range(1, PACK)]
         for number, (t, lo, hi) in enumerate(passes):
             first_acc = bank("first_acc%d" % number, [P, hi - lo], number)
             product(first_acc[:], w1, s1, t, picked_w[:, lo:hi], picked_s[:, lo:hi])
             nc.scalar.activation(out=h[t][:, lo:hi], in_=first_acc[:], func=SILU)
 
-        z_low = low[:].rearrange("p (t c) -> p t c", t=2)
-        z_high = tile("z_high", [P, 7, UNIT], F32)
-        scaled = [keep.tile([P, S], F32, name="scaled%d" % i, tag="scaled%d" % i, align_bytes=64) for i in range(PACK)]
-        z_woven = [tile("z_woven%d" % u, [P, UNIT, PACK], BF16) for u in range(UNITS - 1)]
-
-        def scale(t, lo=0, hi=S):
+        for t, lo, hi in passes:
             lists = task_t[:, lo // 16 : hi // 16]
-            nc.vector.tensor_tensor(scaled[t][:, lo:hi], gam_t[t][:].indirect(lists), h[t][:, lo:hi], MULT)
+            nc.vector.tensor_tensor(scaled[:, t, lo:hi], gam_t[t][:].indirect(lists), h[t][:, lo:hi], MULT)
+        look_up_shift(1, 0, S)
+        look_up_shift(2, 0, S)
+        look_up_shift(3, 0, HALF)
+        deal(nc.scalar.copy, w2[:], w2_raw[:])
+        look_up_shift(3, HALF, S)
+        deal(nc.vector.tensor_copy, s2[:], s2_raw[:])
 
-        def shift(out, t, lo, hi):
-            lists = task_t[:, lo // 16 : hi // 16]
-            nc.vector.tensor_tensor(out, bet_t[t][:].indirect(lists), scaled[t][:, lo:hi], ADD)
-
-        def shift_high(t, half):
-            row = 1 - half if t == 2 else 3 + 2 * half
-            shift(z_high[:, row : row + 2, :].rearrange("p u c -> p (u c)"), t, half * HALF, (half + 1) * HALF)
-
-        def weave_pair(u, pair, src, copy=nc.scalar.copy):
-            copy(out=z_woven[u][:, :, 2 * pair : 2 * pair + 2], in_=src.rearrange("p t c -> p c t"))
-
+        z_woven = [tile("z_woven%d" % u, [P, UNIT, PACK], BF16) for u in range(UNITS)]
         z_w, z_s = tile("z_w", [P, S], U32), tile("z_s", [P, S], U8)
         y_w, y_s = tile("y_w", [P, S], U32), tile("y_s", [P, S], U8)
         y_woven = tile("y_woven", [P, S, PACK], BF16)
-        second_acc = [bank("second_acc%d" % u, [P, PACK, UNIT], u) for u in range(UNITS)]
+        second_acc = [bank("second_acc%d" % u, [P, PACK, UNIT], (len(passes) + u) % 8) for u in range(UNITS)]
 
-        def round_high(u, copy=nc.scalar.copy):
-            row = u + 1 if u < 2 else u - 2
-            weave_pair(u, 1, z_high[:, row : u + 4 : u + 3 - row, :], copy)
+        def in_half(tiles, u):
+            a, lo = divmod(u * UNIT, HALF)
+            return tiles[a][:, :, lo : lo + UNIT]
+
+        def modulate(u):
+            cols = slice(u * UNIT, (u + 1) * UNIT)
+            nc.vector.tensor_tensor(woven(z_woven[u][:]), by_planes(scaled[:, :, cols]), by_planes(shift[:, :, cols]), ADD)
 
         def multiply(u):
             cols = slice(u * UNIT, (u + 1) * UNIT)
@@ -191,58 +183,15 @@ def tile_picked_filmres_silu_po_kernel(
             for t in range(PACK):
                 product(second_acc[u][:, t, :], w2, s2, t, z_w[:, cols], z_s[:, cols])
 
-        scale(0, 0, HALF)
-        scale(0, HALF, S)
-        scale(1)
-        turned_acc = bank("turned_acc", [P, S], len(passes))
-        back_acc = bank("back_acc", [P, S], len(passes) + 1)
-        turned = tile("turned", [P, S], F32)
-        for u in range(UNITS):
-            cols = slice(u * UNIT, (u + 1) * UNIT)
-            for k, term in enumerate((shift0, scaled[0])):
-                nc.tensor.matmul(
-                    turned_acc[:, cols], lhsT=term[:, cols], rhs=identity[:], is_transpose=True, start=k == 0, stop=k == 1
-                )
-        nc.scalar.copy(out=turned[:], in_=turned_acc[:])
-        w2 = keep.tile([P, W], I32, name="w2", tag="shift0", align_bytes=64)
-        deal_words(w2[:], w2_raw[:])
-        for u in range(UNITS):
-            cols = slice(u * UNIT, (u + 1) * UNIT)
-            nc.tensor.transpose(back_acc[:, cols], turned[:, cols], identity[:])
-        nc.scalar.copy(out=z_low[:, 0, 0 : S - UNIT], in_=back_acc[:, 0 : S - UNIT])
-        scale(2)
-        shift(z_low[:, 1, 0:S], 1, 0, S)
-        scale(LAST)
-        for u in range(UNITS - 1):
-            if u == 2:
-                nc.scalar.copy(out=z_low[:, 0, S - UNIT : S], in_=back_acc[:, S - UNIT : S])
-            weave_pair(u, 0, z_low[:, :, u * UNIT : (u + 1) * UNIT])
-        shift_high(2, 0)
-        shift_high(LAST, 0)
-        shift_high(LAST, 1)
-        deal(s2[:], s2_raw[:])
-        warm_acc = bank("warm_acc", [P, S], len(passes) + 1)
-        for t in range(2):
-            product(warm_acc[:], w1, s1, t, picked_w[:], picked_s[:])
-        round_high(0)
-        round_high(1)
-        z_woven.append(keep.tile([P, UNIT, PACK], BF16, name="z_woven3", tag="scaled3", align_bytes=64))
-        weave_pair(UNITS - 1, 0, z_low[:, :, S - UNIT : S])
-        multiply(0)
-        shift_high(2, 1)
-        round_high(3)
-        multiply(1)
-        round_high(2, nc.vector.tensor_copy)
-
         def add_residual(u):
             cols = slice(u * UNIT, (u + 1) * UNIT)
             y = tile("y%d" % u, [P, PACK, UNIT], F32)
-            nc.vector.tensor_tensor(y[:], second_acc[u][:], res_t[:, :, cols], ADD)
+            nc.vector.tensor_tensor(y[:], second_acc[u][:], in_half(res_t, u), ADD)
             nc.sync.dma_start(out=planes_of(out_0)[:, :, cols], in_=y[:])
             share = LAST_SHARE if u == UNITS - 1 else UNIT
-            weave(nc.scalar.copy, y_woven[:, u * UNIT : u * UNIT + share, :], y[:, :, 0:share])
+            nc.scalar.copy(out=woven(y_woven[:, u * UNIT : u * UNIT + share, :]), in_=by_planes(y[:, :, 0:share]))
             if share < UNIT:
-                weave(nc.vector.tensor_copy, y_woven[:, u * UNIT + share : S, :], y[:, :, share:UNIT])
+                nc.vector.tensor_copy(out=woven(y_woven[:, u * UNIT + share : S, :]), in_=by_planes(y[:, :, share:UNIT]))
 
         def hand_on(lo, hi):
             cols = slice(lo, hi)
@@ -251,10 +200,12 @@ def tile_picked_filmres_silu_po_kernel(
         def store_words(lo, hi):
             nc.sync.dma_start(out=words_of(out_1)[:, lo:hi], in_=y_w[:, lo:hi].bitcast(I32))
 
-        add_residual(0)
-        multiply(2)
-        multiply(3)
-        for u in range(1, UNITS):
+        for a in range(2):
+            modulate(2 * a)
+            modulate(2 * a + 1)
+            multiply(2 * a)
+            multiply(2 * a + 1)
+        for u in range(UNITS):
             add_residual(u)
         hand_on(0, HALF)
         hand_on(HALF, S - UNIT)

@@ -24,7 +24,8 @@ W = 512
 HALF = S // 2
 UNIT = 128
 UNITS = S // UNIT
-LAST_SHARE = 32
+LAST_SHARE = 48
+X_FIRST = 768
 FLOPS = 2 * 2 * 512 * 512 * 512
 
 
@@ -54,10 +55,10 @@ def tile_picked_filmres_silu_po_kernel(
         )
 
     def woven(ap):
-        return ap.rearrange("p (c i) t -> p c t i", i=4)
+        return ap.rearrange("p (c i) t -> p c t i", i=2)
 
     def by_planes(ap):
-        return ap.rearrange("p t (c i) -> p c t i", i=4)
+        return ap.rearrange("p t (c i) -> p c t i", i=2)
 
     def product(acc, weights, weight_scales, t, codes, scales):
         rows = slice(t * P, (t + 1) * P)
@@ -107,15 +108,14 @@ def tile_picked_filmres_silu_po_kernel(
         def load_plane(tiles, dram, t):
             nc.sync.dma_start(out=tiles[t][:, 0:W], in_=planes_of(dram)[:, t, :])
 
-        def load_x_half(a):
-            cols = slice(a * TOKENS // 2, (a + 1) * TOKENS // 2)
-            nc.sync.dma_start(out=x_w[:].bitcast(I32)[:, cols], in_=words_of(x_words)[:, cols])
+        def load_x(lo, hi):
+            nc.sync.dma_start(out=x_w[:].bitcast(I32)[:, lo:hi], in_=words_of(x_words)[:, lo:hi])
 
         nc.sync.dma_start(offs_t[:], offs)
         nc.sync.dma_start(task_t[:], task)
-        load_x_half(0)
+        load_x(0, X_FIRST)
         load_scales(x_s, x_scales)
-        load_x_half(1)
+        load_x(X_FIRST, TOKENS)
         nc.sync.dma_start(out=w1_raw[:].bitcast(I32), in_=words_of(w1_words))
         load_scales(s1_raw, w1_scales)
         for tiles, dram, t in ((bet_t, bet, 0), (gam_t, gam, 0), (gam_t, gam, 1)):
@@ -190,8 +190,7 @@ def tile_picked_filmres_silu_po_kernel(
             nc.sync.dma_start(out=planes_of(out_0)[:, :, cols], in_=y[:])
             share = LAST_SHARE if u == UNITS - 1 else UNIT
             nc.scalar.copy(out=woven(y_woven[:, u * UNIT : u * UNIT + share, :]), in_=by_planes(y[:, :, 0:share]))
-            if share < UNIT:
-                nc.vector.tensor_copy(out=woven(y_woven[:, u * UNIT + share : S, :]), in_=by_planes(y[:, :, share:UNIT]))
+            return y
 
         def hand_on(lo, hi):
             cols = slice(lo, hi)
@@ -205,9 +204,11 @@ def tile_picked_filmres_silu_po_kernel(
             modulate(2 * a + 1)
             multiply(2 * a)
             multiply(2 * a + 1)
-        for u in range(UNITS):
-            add_residual(u)
+        y_last = [add_residual(u) for u in range(UNITS)][-1]
         hand_on(0, HALF)
+        nc.vector.tensor_copy(
+            out=woven(y_woven[:, S - UNIT + LAST_SHARE : S, :]), in_=by_planes(y_last[:, :, LAST_SHARE:UNIT])
+        )
         hand_on(HALF, S - UNIT)
         store_words(0, S - UNIT)
         hand_on(S - UNIT, S)

@@ -18,6 +18,8 @@ P = 128
 PACK = 4
 QUAD = 32
 ROWS = 4
+W1_ROW = ROWS
+W2_ROW = 2 * ROWS
 TOKENS = 2048
 S = 512
 W = 512
@@ -25,7 +27,7 @@ HALF = S // 2
 UNIT = 128
 UNITS = S // UNIT
 LAST_SHARE = 48
-X_FIRST = 768
+X_FIRST = 896
 FLOPS = 2 * 2 * 512 * 512 * 512
 
 
@@ -41,7 +43,7 @@ def tile_picked_filmres_silu_po_kernel(
         return dram.rearrange("(p t) c -> p t c", t=PACK)
 
     def scale_rows(plane, dram, r):
-        return plane[r:P:QUAD, :].bitcast(I32), dram[0, r : ROWS * P // QUAD : ROWS, :].bitcast(I32)
+        return plane[r : P - 3 * ROWS : QUAD, :].bitcast(I32), dram[0, r : ROWS * P // QUAD : ROWS, :].bitcast(I32)
 
     def load_scales(plane, dram, lo=0, hi=ROWS):
         for r in range(lo, hi):
@@ -111,18 +113,18 @@ def tile_picked_filmres_silu_po_kernel(
         def load_x(lo, hi):
             nc.sync.dma_start(out=x_w[:].bitcast(I32)[:, lo:hi], in_=words_of(x_words)[:, lo:hi])
 
+        load_x(0, X_FIRST)
         nc.sync.dma_start(offs_t[:], offs)
         nc.sync.dma_start(task_t[:], task)
-        load_x(0, X_FIRST)
         load_scales(x_s, x_scales)
         load_x(X_FIRST, TOKENS)
         nc.sync.dma_start(out=w1_raw[:].bitcast(I32), in_=words_of(w1_words))
-        load_scales(s1_raw, w1_scales)
+        load_scales(s1_raw[W1_ROW:P, :], w1_scales)
         for tiles, dram, t in ((bet_t, bet, 0), (gam_t, gam, 0), (gam_t, gam, 1)):
             load_plane(tiles, dram, t)
         for r, (tiles, dram, t) in enumerate(((gam_t, gam, 2), (gam_t, gam, 3), (bet_t, bet, 1), (bet_t, bet, 2))):
             load_plane(tiles, dram, t)
-            load_scales(s2_raw, w2_scales, r, r + 1)
+            load_scales(s2_raw[W2_ROW:P, :], w2_scales, r, r + 1)
         load_plane(bet_t, bet, 3)
         nc.sync.dma_start(out=w2_raw[:].bitcast(I32), in_=words_of(w2_words))
         for a in range(2):
@@ -150,7 +152,7 @@ def tile_picked_filmres_silu_po_kernel(
         passes = [(0, 0, HALF), (0, HALF, S)] + [(t, 0, S) for t in range(1, PACK)]
         for number, (t, lo, hi) in enumerate(passes):
             first_acc = bank("first_acc%d" % number, [P, hi - lo], number)
-            product(first_acc[:], w1, s1, t, picked_w[:, lo:hi], picked_s[:, lo:hi])
+            product(first_acc[:], w1, s1[W1_ROW:P, :], t, picked_w[:, lo:hi], picked_s[:, lo:hi])
             nc.scalar.activation(out=h[t][:, lo:hi], in_=first_acc[:], func=SILU)
 
         for t, lo, hi in passes:
@@ -181,7 +183,7 @@ def tile_picked_filmres_silu_po_kernel(
             cols = slice(u * UNIT, (u + 1) * UNIT)
             quantise(z_w[:, cols], z_s[:, cols], z_woven[u][:])
             for t in range(PACK):
-                product(second_acc[u][:, t, :], w2, s2, t, z_w[:, cols], z_s[:, cols])
+                product(second_acc[u][:, t, :], w2, s2[W2_ROW:P, :], t, z_w[:, cols], z_s[:, cols])
 
         def add_residual(u):
             cols = slice(u * UNIT, (u + 1) * UNIT)

@@ -160,7 +160,8 @@ def tile_picked_filmres_silu_po_kernel(
             nc.vector.tensor_tensor(scaled[:, t, lo:hi], gam_t[t][:].indirect(lists), h[t][:, lo:hi], MULT)
         look_up_shift(1, 0, S)
         look_up_shift(2, 0, S)
-        look_up_shift(3, 0, HALF)
+        look_up_shift(3, 0, UNIT)
+        look_up_shift(3, UNIT, HALF)
         deal(nc.scalar.copy, w2[:], w2_raw[:])
         look_up_shift(3, HALF, S)
         deal(nc.vector.tensor_copy, s2[:], s2_raw[:])

from contextlib import ExitStack

import concourse.mybir as mybir

F32 = mybir.dt.float32
BF16 = mybir.dt.bfloat16
I32 = mybir.dt.int32
U32 = mybir.dt.uint32
U16 = mybir.dt.uint16
U8 = mybir.dt.uint8
FP8X4 = mybir.dt.float8_e4m3fn_x4
MULT = mybir.AluOpType.mult
ADD = mybir.AluOpType.add
SILU = mybir.ActivationFunctionType.Silu
COPY = mybir.ActivationFunctionType.Copy

P = 128
PACK = 4
QUAD = 32
ROWS = 4
W1_ROW = ROWS
W2_ROW = 2 * ROWS
TOKENS = 2048
S = 512
W = 512
HALF = S // 2
UNIT = 128
UNITS = S // UNIT
LAST_SHARE = 48
X_FIRST = 896
FLOPS = 2 * 2 * 512 * 512 * 512


def tile_picked_filmres_silu_po_kernel(
    tc, x_words, x_scales, w1_words, w1_scales, gam, bet, res, w2_words, w2_scales, offs, task, out_0, out_1, out_2
):
    nc = tc.nc

    def words_of(dram):
        return dram[0].rearrange("p n t -> p (n t)").bitcast(I32)

    def planes_of(dram):
        return dram.rearrange("(p t) c -> p t c", t=PACK)

    def scale_rows(plane, dram, r):
        return plane[r : P - 3 * ROWS : QUAD, :].bitcast(I32), dram[0, r : ROWS * P // QUAD : ROWS, :].bitcast(I32)

    def load_scales(plane, dram, lo=0, hi=ROWS):
        for r in range(lo, hi):
            rows, source = scale_rows(plane, dram, r)
            nc.sync.dma_start(out=rows, in_=source)

    def deal(copy, dst, src, lo=0, hi=PACK):
        copy(
            out=dst.rearrange("p (t m) -> p m t", t=PACK)[:, :, lo:hi],
            in_=src.rearrange("p (m t) -> p m t", t=PACK)[:, :, lo:hi],
        )

    def woven(ap):
        return ap.rearrange("p (c i) t -> p c t i", i=2)

    def by_planes(ap):
        return ap.rearrange("p t (c i) -> p c t i", i=2)

    def product(acc, weights, weight_scales, t, codes, scales):
        rows = slice(t * P, (t + 1) * P)
        nc.tensor.matmul_mx(
            out=acc,
            lhsT=weights[:, rows].bitcast(FP8X4),
            lhsT_scale=weight_scales[:, rows],
            rhs=codes.bitcast(FP8X4),
            rhs_scale=scales,
            start=True,
            stop=True,
        )

    def quantise(codes, scales, rounded):
        nc.vector.quantize_mx(out=codes.bitcast(FP8X4), scales=scales, in_=rounded.rearrange("p c t -> p (c t)"))

    with ExitStack() as ctx:
        keep = ctx.enter_context(tc.tile_pool(name="keep", bufs=1))
        psum = ctx.enter_context(tc.psum_pool(name="psum", bufs=1))

        def tile(name, shape, dtype):
            return keep.tile(shape, dtype, name=name, align_bytes=64)

        def bank(name, shape, number):
            return psum.tile(shape, F32, name=name, tag="bank%d" % number)

        offs_t = tile("offs_t", [P, S // 16], U16)
        task_t = tile("task_t", [P, S // 16], U16)
        x_w = tile("x_w", [P, TOKENS], U32)
        x_s = tile("x_s", [P, TOKENS], U8)
        w1_raw = tile("w1_raw", [P, W], U32)
        w2_raw = tile("w2_raw", [P, W], U32)
        s1_raw = tile("s1_raw", [P, W], U8)
        s2_raw = tile("s2_raw", [P, W], U8)
        res_t = [tile("res%d" % a, [P, PACK, HALF], F32) for a in range(2)]
        gam_t = [tile("gam%d" % t, [P, 2 * W], F32) for t in range(PACK)]
        bet_t = [tile("bet%d" % t, [P, W if t == PACK - 1 else 2 * W], F32) for t in range(PACK)]

        nc.vector.memset(x_s[:].bitcast(I32), 0)
        nc.vector.memset(s1_raw[:].bitcast(I32), 0)
        nc.vector.memset(s2_raw[:].bitcast(I32), 0)
        zero = tile("zero", [P, 1], F32)
        first = tile("first", [P, 1], F32)
        nc.vector.memset(zero[:], 0.0)
        nc.scalar.activation(out=first[:], in_=zero[:], func=SILU)

        def load_plane(tiles, dram, t):
            nc.sync.dma_start(out=tiles[t][:, 0:W], in_=planes_of(dram)[:, t, :])

        def load_x(lo, hi):
            nc.sync.dma_start(out=x_w[:].bitcast(I32)[:, lo:hi], in_=words_of(x_words)[:, lo:hi])

        load_x(0, X_FIRST)
        nc.sync.dma_start(offs_t[:], offs)
        nc.sync.dma_start(task_t[:], task)
        load_scales(x_s, x_scales)
        load_x(X_FIRST, TOKENS)
        nc.sync.dma_start(out=w1_raw[:].bitcast(I32), in_=words_of(w1_words))
        load_scales(s1_raw[W1_ROW:P, :], w1_scales)
        for tiles, dram, t in ((bet_t, bet, 0), (gam_t, gam, 0), (gam_t, gam, 1)):
            load_plane(tiles, dram, t)
        for r, (tiles, dram, t) in enumerate(((gam_t, gam, 2), (gam_t, gam, 3), (bet_t, bet, 1), (bet_t, bet, 2))):
            load_plane(tiles, dram, t)
            load_scales(s2_raw[W2_ROW:P, :], w2_scales, r, r + 1)
        load_plane(bet_t, bet, 3)
        nc.sync.dma_start(out=w2_raw[:].bitcast(I32), in_=words_of(w2_words))
        for a in range(2):
            nc.sync.dma_start(out=res_t[a][:], in_=planes_of(res)[:, :, a * HALF : (a + 1) * HALF])

        picked_s = tile("picked_s", [P, S], U8)
        picked_w = tile("picked_w", [P, S], U32)
        w1, s1 = tile("w1", [P, W], U32), tile("s1", [P, W], U8)
        w2, s2 = tile("w2", [P, W], U32), tile("s2", [P, W], U8)
        nc.vector.tensor_copy(picked_s[:], x_s[:].indirect(offs_t[:]))
        nc.vector.tensor_copy(picked_w[:], x_w[:].indirect(offs_t[:]))
        deal(nc.vector.tensor_copy, s1[:], s1_raw[:], 0, 1)
        deal(nc.vector.tensor_copy, s1[:], s1_raw[:], 1, PACK)
        deal(nc.scalar.copy, w1[:], w1_raw[:], 0, 1)
        deal(nc.scalar.copy, w1[:], w1_raw[:], 1, PACK)
        scaled = tile("scaled", [P, PACK * S], F32)[:].rearrange("p (t c) -> p t c", t=PACK)
        shift = tile("shift", [P, PACK * S], F32)[:].rearrange("p (t c) -> p t c", t=PACK)

        def look_up_shift(t, lo, hi):
            nc.scalar.activation(shift[:, t, lo:hi], bet_t[t][:].indirect(task_t[:, lo // 16 : hi // 16]), COPY)

        nc.vector.tensor_copy(shift[:, 0, :], bet_t[0][:].indirect(task_t[:]))

        h = [tile("h%d" % t, [P, S], F32) for t in range(PACK)]
        passes = [(0, 0, HALF), (0, HALF, S)] + [(t, 0, S) for t in range(1, PACK)]
        for number, (t, lo, hi) in enumerate(passes):
            first_acc = bank("first_acc%d" % number, [P, hi - lo], number)
            product(first_acc[:], w1, s1[W1_ROW:P, :], t, picked_w[:, lo:hi], picked_s[:, lo:hi])
            nc.scalar.activation(out=h[t][:, lo:hi], in_=first_acc[:], func=SILU)

        for t, lo, hi in passes:
            lists = task_t[:, lo // 16 : hi // 16]
            nc.vector.tensor_tensor(scaled[:, t, lo:hi], gam_t[t][:].indirect(lists), h[t][:, lo:hi], MULT)
        look_up_shift(1, 0, S)
        look_up_shift(2, 0, S)
        look_up_shift(3, 0, UNIT)
        look_up_shift(3, UNIT, HALF)
        deal(nc.scalar.copy, w2[:], w2_raw[:])
        look_up_shift(3, HALF, S)
        deal(nc.vector.tensor_copy, s2[:], s2_raw[:])

        z_woven = [tile("z_woven%d" % u, [P, UNIT, PACK], BF16) for u in range(UNITS)]
        z_w, z_s = tile("z_w", [P, S], U32), tile("z_s", [P, S], U8)
        y_w, y_s = tile("y_w", [P, S], U32), tile("y_s", [P, S], U8)
        y_woven = tile("y_woven", [P, S, PACK], BF16)
        second_acc = [bank("second_acc%d" % u, [P, PACK, UNIT], (len(passes) + u) % 8) for u in range(UNITS)]

        def in_half(tiles, u):
            a, lo = divmod(u * UNIT, HALF)
            return tiles[a][:, :, lo : lo + UNIT]

        def modulate(u):
            cols = slice(u * UNIT, (u + 1) * UNIT)
            nc.vector.tensor_tensor(woven(z_woven[u][:]), by_planes(scaled[:, :, cols]), by_planes(shift[:, :, cols]), ADD)

        def multiply(u):
            cols = slice(u * UNIT, (u + 1) * UNIT)
            quantise(z_w[:, cols], z_s[:, cols], z_woven[u][:])
            for t in range(PACK):
                product(second_acc[u][:, t, :], w2, s2[W2_ROW:P, :], t, z_w[:, cols], z_s[:, cols])

        def add_residual(u):
            cols = slice(u * UNIT, (u + 1) * UNIT)
            y = tile("y%d" % u, [P, PACK, UNIT], F32)
            nc.vector.tensor_tensor(y[:], second_acc[u][:], in_half(res_t, u), ADD)
            nc.sync.dma_start(out=planes_of(out_0)[:, :, cols], in_=y[:])
            share = LAST_SHARE if u == UNITS - 1 else UNIT
            nc.scalar.copy(out=woven(y_woven[:, u * UNIT : u * UNIT + share, :]), in_=by_planes(y[:, :, 0:share]))
            return y

        def hand_on(lo, hi):
            cols = slice(lo, hi)
            quantise(y_w[:, cols], y_s[:, cols], y_woven[:, cols, :])

        def store_words(lo, hi):
            nc.sync.dma_start(out=words_of(out_1)[:, lo:hi], in_=y_w[:, lo:hi].bitcast(I32))

        for a in range(2):
            modulate(2 * a)
            modulate(2 * a + 1)
            multiply(2 * a)
            multiply(2 * a + 1)
        y_last = [add_residual(u) for u in range(UNITS)][-1]
        hand_on(0, HALF)
        nc.vector.tensor_copy(
            out=woven(y_woven[:, S - UNIT + LAST_SHARE : S, :]), in_=by_planes(y_last[:, :, LAST_SHARE:UNIT])
        )
        hand_on(HALF, S - UNIT)
        store_words(0, S - UNIT)
        hand_on(S - UNIT, S)
        store_words(S - UNIT, S)
        for r in range(ROWS):
            rows, target = scale_rows(y_s, out_2, r)
            (nc.sync if r == 0 else nc.scalar).dma_start(out=target, in_=rows)
